import numpy as np
import ml_dtypes


def mxq(x, axis, fmt="e4m3"):
    dtype, down = {"e4m3": (ml_dtypes.float8_e4m3fn, 7), "e5m2": (ml_dtypes.float8_e5m2, 14)}[fmt]
    v = np.moveaxis(np.asarray(x, np.float32).astype(ml_dtypes.bfloat16).astype(np.float64), axis, -1)
    blocks = v.reshape(v.shape[:-1] + (-1, 32))
    amax = np.abs(blocks).max(-1, keepdims=True)
    byte = np.maximum(np.where(amax > 0, np.frexp(amax)[1] - 1 + 127, 0) - down, 1)
    scale = np.exp2(byte - 127.0)
    codes = (blocks / scale).astype(np.float32).astype(dtype).astype(np.float64)
    return np.moveaxis((codes * scale).reshape(v.shape), -1, axis)


WIDE = False


def mx_kscale(k):
    if not WIDE:
        return np.ones(k)
    levels = np.array([10, -10, 5, -5, 0])
    if k % 512:
        return np.exp2(np.random.permutation(np.resize(levels, k // 32))).repeat(32)
    a = np.empty((k // 512, 16))
    for p in range(k // 512):
        a[p, :8] = np.random.permutation(np.resize(levels, 8))
        for g in range(8):
            far = levels[np.abs(levels - a[p, g]) >= 10]
            a[p, g + 8] = far[np.random.randint(len(far))]
    return np.exp2(a.ravel()).repeat(32)


def f64(x):
    return np.asarray(x).astype(np.float64)


def striped(idx):
    return np.tile(idx.reshape(-1, 16).T, (8, 1)).astype(np.uint16)


def unstriped(offs):
    return offs[:16].T.reshape(-1).astype(np.int64)


E2M1 = np.array([0.0, 0.5, 1.0, 1.5, 2.0, 3.0, 4.0, 6.0, -0.0, -0.5, -1.0, -1.5, -2.0, -3.0, -4.0, -6.0])


def pack_weight(w, fmt):
    k, n = w.shape
    w = f64(np.asarray(w, np.float32).astype(ml_dtypes.bfloat16)).reshape(k // 32, 32, n)
    amax = np.abs(w).max(1)
    if fmt == "e4m3":
        byte = np.frexp(amax)[1] - 1 + 127 - 7
    else:
        mant, ex = np.frexp(amax / 6.0)
        byte = np.where(mant > 0.5, ex, ex - 1) + 127
    byte = np.clip(np.where(amax > 0, byte, 1), 1, 254)
    scaled = (w * np.exp2(127.0 - byte)[:, None, :]).reshape(k, n).astype(np.float32)
    by_word = np.ascontiguousarray(scaled.reshape(k // 512, 128, 4, n).transpose(0, 1, 3, 2))
    if fmt == "e4m3":
        words = by_word.astype(ml_dtypes.float8_e4m3fn).view(np.uint8)
    else:
        c = by_word.astype(ml_dtypes.float4_e2m1fn).view(np.uint8) & 0xF
        words = (c[..., 0::2] | (c[..., 1::2] << 4)).reshape(k // 512, 128, 2 * n)
    return np.ascontiguousarray(words), np.ascontiguousarray(byte.astype(np.uint8).reshape(k // 512, 16, n))


def unpack_weight(words, scales, fmt):
    g, _, n = scales.shape
    words = np.ascontiguousarray(words).reshape(g, 128, n, -1)
    if fmt == "e4m3":
        vals = words.view(ml_dtypes.float8_e4m3fn).astype(np.float64)
    else:
        nib = np.empty((g, 128, n, 4), np.uint8)
        nib[..., 0::2] = words & 0xF
        nib[..., 1::2] = words >> 4
        vals = E2M1[nib]
    vals = vals * np.repeat(np.exp2(scales.astype(np.float64) - 127.0), 8, axis=1)[..., None]
    return vals.transpose(0, 1, 3, 2).reshape(g * 512, n)


def gelu(v):
    return 0.5 * v * (1.0 + np.tanh(np.sqrt(2.0 / np.pi) * (v + 0.044715 * v**3)))


K, T, H, N, S, T2 = 1024, 2048, 1024, 512, 1024, 2048

def setup_inputs():
    n = np.random.standard_normal
    s = mx_kscale(K)[:, None]
    u = mx_kscale(H)[:, None]
    tab_words, tab_scales = pack_weight(n((K, T)) * s, "e4m3")
    w4_words, w4_scales = pack_weight(n((H, N)) / np.sqrt(H) / u, "e2m1")
    return {
        "tab_words": tab_words, "tab_scales": tab_scales,
        "offs": striped(np.random.permutation(T)[:S]),
        "load": (0.5 * n((K, H)) / np.sqrt(K) / s).astype(np.float32),
        "drift": (0.2 * n(H)).astype(np.float32),
        "price": (np.exp(0.3 * n(H)) * u[:, 0]).astype(np.float32),
        "w4_words": w4_words, "w4_scales": w4_scales,
        "wgo": np.exp(0.3 * n((128, S))).astype(np.float32),
        "offs2": striped(np.random.permutation(T2)[:S]),
    }

def reference(tab_words, tab_scales, offs, load, drift, price, w4_words, w4_scales, wgo, offs2):
    v = unpack_weight(tab_words, tab_scales, "e4m3")[:, unstriped(offs)]
    l = mxq(f64(load), 0, "e4m3")
    w4 = unpack_weight(w4_words, w4_scales, "e2m1")
    r = (l.T @ v) + f64(drift)[:, None]
    h = f64(price)[:, None] * (np.exp(r) - 1.0)
    y = w4.T @ mxq(h, 0, "e4m3")
    out = np.zeros((N, T2))
    out[:, unstriped(offs2)] = np.tile(f64(wgo), (N // 128, 1)) * y
    return out

@@ -1,0 +1,261 @@
+from contextlib import ExitStack
+
+import concourse.mybir as mybir
+
+K, T, H, N, S, T2 = 1024, 2048, 1024, 512, 1024, 2048
+FLOPS = 2 * K * H * S + 2 * H * N * S
+
+F32 = mybir.dt.float32
+BF16 = mybir.dt.bfloat16
+I32 = mybir.dt.int32
+U32 = mybir.dt.uint32
+U16 = mybir.dt.uint16
+U8 = mybir.dt.uint8
+FP8X4 = mybir.dt.float8_e4m3fn_x4
+FP4X4 = mybir.dt.float4_e2m1fn_x4
+ALU = mybir.AluOpType
+ACT = mybir.ActivationFunctionType
+
+P = 128
+PACK = 4
+KP = P * PACK
+CHUNKS = [(0, 256), (256, 256), (512, 512)]
+
+
+def tile_list_scenario_profit_store_kernel(
+    tc, tab_words, tab_scales, offs, load, drift, price, w4_words, w4_scales, wgo, offs2, out
+):
+    nc = tc.nc
+    with ExitStack() as ctx:
+        keep = ctx.enter_context(tc.tile_pool(name="keep", bufs=1))
+        psum_r = ctx.enter_context(tc.psum_pool(name="psum_r", bufs=5))
+        psum_y = ctx.enter_context(tc.psum_pool(name="psum_y", bufs=3))
+
+        def sb(shape, dtype, name):
+            return keep.tile(shape, dtype, name=name, align_bytes=64)
+
+        gather_list = sb([P, S // 16], U16, "gather_list")
+        scatter_list = sb([P, S // 16], U16, "scatter_list")
+        tab_w = [sb([P, T], I32, "tab_w%d" % a) for a in range(2)]
+        tab_s = sb([P, T], U8, "tab_s")
+        raw = {(a, b): sb([P, PACK, KP], F32, "raw%d%d" % (a, b)) for a in range(2) for b in range(2)}
+        grouped = {ab: sb([P, PACK * KP], BF16, "grouped%d%d" % ab) for ab in raw}
+        l_codes = {ab: sb([P, KP], U32, "l_codes%d%d" % ab) for ab in raw}
+        l_scales = {ab: sb([P, KP], U8, "l_scales%d%d" % ab) for ab in raw}
+        drift_sb = sb([P, 2, PACK], F32, "drift_sb")
+        price_sb = sb([P, 2, PACK], F32, "price_sb")
+        minus_price = sb([P, 2, PACK], F32, "minus_price")
+        w4_w = sb([P, 2, 2 * N], U8, "w4_w")
+        w4_s = sb([P, 2, N], U8, "w4_s")
+        wgo_sb = [sb([P, w], F32, "wgo%d" % c) for c, (j0, w) in enumerate(CHUNKS)]
+        windows = [sb([P, T2], F32, "window%d" % n) for n in range(N // P)]
+        v_codes = {(a, c): sb([P, w], U32, "v_codes%d%d" % (a, c)) for a in range(2) for c, (j0, w) in enumerate(CHUNKS)}
+        v_scales = [sb([P, w], U8, "v_scales%d" % c) for c, (j0, w) in enumerate(CHUNKS)]
+        warm = sb([P, 1], F32, "warm")
+        warm_out = sb([P, 1], F32, "warm_out")
+
+        def list_cols(c):
+            j0, w = CHUNKS[c]
+            return slice(j0 // 16, (j0 + w) // 16)
+
+        nc.vector.memset(tab_s[:].bitcast(I32), 0)
+        nc.vector.memset(warm[:], 0.0)
+        nc.scalar.activation(warm_out[:], warm[:], ACT.Exp)
+        nc.vector.memset(w4_s[:].rearrange("p b n -> p (b n)").bitcast(I32), 0)
+        for n in range(N // P):
+            nc.vector.memset(windows[n][:], 0.0)
+
+        def load_table_words(a):
+            nc.sync.dma_start(tab_w[a][:], tab_words[a].rearrange("p t i -> p (t i)").bitcast(I32))
+
+        def load_table_scales(a):
+            for q in range(4):
+                row = 32 * q + 4 * a
+                nc.sync.dma_start(
+                    tab_s[row : row + 4, :].bitcast(I32), tab_scales[a, 4 * q : 4 * q + 4, :].bitcast(I32)
+                )
+
+        def load_loadings(a, b, c0, c1):
+            rows = load[KP * a : KP * (a + 1), KP * b + c0 : KP * b + c1]
+            nc.sync.dma_start(raw[a, b][:, :, c0:c1], rows.rearrange("(p j) c -> p j c", j=PACK))
+
+        nc.sync.dma_start(gather_list[:], offs)
+        load_table_words(0)
+        load_table_scales(0)
+        load_loadings(0, 0, 0, KP)
+        load_table_scales(1)
+        load_table_words(1)
+        load_loadings(1, 0, 0, KP)
+        nc.sync.dma_start(drift_sb[:], drift.rearrange("(b p t) -> p b t", b=2, t=PACK))
+        nc.sync.dma_start(price_sb[:], price.rearrange("(b p t) -> p b t", b=2, t=PACK))
+        load_loadings(0, 1, 0, KP)
+        load_loadings(1, 1, 0, KP // 2)
+        load_loadings(1, 1, KP // 2, KP)
+        nc.sync.dma_start(w4_w[:].bitcast(I32), w4_words.rearrange("b p c -> p b c").bitcast(I32))
+        for q in range(4):
+            nc.sync.dma_start(
+                w4_s[32 * q : 32 * q + 4, :, :].bitcast(I32),
+                w4_scales[:, 4 * q : 4 * q + 4, :].rearrange("b r n -> r b n").bitcast(I32),
+            )
+        nc.sync.dma_start(scatter_list[:], offs2)
+        for c, (j0, w) in enumerate(CHUNKS):
+            nc.sync.dma_start(wgo_sb[c][:], wgo[:, j0 : j0 + w])
+
+        def gather_words(a, c):
+            nc.vector.tensor_copy(v_codes[a, c][:], tab_w[a][:].bitcast(U32).indirect(gather_list[:, list_cols(c)]))
+
+        def gather_scales(c):
+            nc.vector.tensor_copy(v_scales[c][:], tab_s[:].indirect(gather_list[:, list_cols(c)]))
+
+        def round_loadings(copy, a, b, m0, m1):
+            copy(
+                grouped[a, b][:].rearrange("p (t m j) -> p m j t", t=PACK, j=PACK)[:, m0:m1],
+                raw[a, b][:].rearrange("p j (m t) -> p m j t", t=PACK)[:, m0:m1],
+            )
+
+        def quantise_loadings(a, b, t0, t1):
+            nc.vector.quantize_mx(
+                out=l_codes[a, b][:, P * t0 : P * t1].bitcast(FP8X4),
+                scales=l_scales[a, b][:, P * t0 : P * t1],
+                in_=grouped[a, b][:, KP * t0 : KP * t1],
+            )
+
+        growth = {}
+        h_grouped = {}
+        h_codes = {}
+        h_scales = {}
+
+        def returns(b, c):
+            w = CHUNKS[c][1]
+            growth[b, c] = sb([P, PACK, w], F32, "growth%d%d" % (b, c))
+            for t in range(PACK):
+                r = psum_r.tile([P, KP], F32, name="r")
+                for a in range(2):
+                    nc.tensor.matmul_mx(
+                        out=r[:, :w],
+                        lhsT=l_codes[a, b][:, P * t : P * (t + 1)].bitcast(FP8X4),
+                        lhsT_scale=l_scales[a, b][:, P * t : P * (t + 1)],
+                        rhs=v_codes[a, c][:].bitcast(FP8X4),
+                        rhs_scale=v_scales[c][4 * a : P, :],
+                        start=(a == 0),
+                        stop=(a == 1),
+                    )
+                nc.scalar.activation(growth[b, c][:, t, :], r[:, :w], ACT.Exp, bias=drift_sb[:, b, t : t + 1])
+
+        def profit_on_vector(b, c):
+            w = CHUNKS[c][1]
+            h_grouped[b, c] = sb([P, w, PACK], BF16, "h_grouped%d%d" % (b, c))
+            nc.vector.scalar_tensor_tensor(
+                h_grouped[b, c][:],
+                growth[b, c][:].rearrange("p t j -> p j t"),
+                -1.0,
+                price_sb[:, b, :].unsqueeze(1).to_broadcast([P, w, PACK]),
+                ALU.add,
+                ALU.mult,
+            )
+
+        def profit_on_scalar(b, c):
+            w = CHUNKS[c][1]
+            planes = sb([P, PACK, w], BF16, "h_planes%d%d" % (b, c))
+            h_grouped[b, c] = sb([P, w, PACK], BF16, "h_grouped%d%d" % (b, c))
+            for t in range(PACK):
+                nc.scalar.activation(
+                    planes[:, t, :],
+                    growth[b, c][:, t, :],
+                    ACT.Identity,
+                    bias=minus_price[:, b, t : t + 1],
+                    scale=price_sb[:, b, t : t + 1],
+                )
+            nc.scalar.copy(
+                h_grouped[b, c][:].rearrange("p (g i) t -> p g t i", i=4),
+                planes[:].rearrange("p t (g i) -> p g t i", i=4),
+            )
+
+        def quantise_profit(b, c):
+            w = CHUNKS[c][1]
+            h_codes[b, c] = sb([P, w], U32, "h_codes%d%d" % (b, c))
+            h_scales[b, c] = sb([P, w], U8, "h_scales%d%d" % (b, c))
+            nc.vector.quantize_mx(
+                out=h_codes[b, c][:].bitcast(FP8X4),
+                scales=h_scales[b, c][:],
+                in_=h_grouped[b, c][:].rearrange("p j t -> p (j t)"),
+            )
+
+        y_sb = {}
+
+        def portfolios(n, c):
+            w = CHUNKS[c][1]
+            step = KP if w == KP else P
+            y = psum_y.tile([P, KP], F32, name="y")
+            for j0 in range(0, w, step):
+                for b in range(2):
+                    nc.tensor.matmul_mx(
+                        out=y[:, j0 : j0 + step],
+                        lhsT=w4_w[:, b, 2 * P * n : 2 * P * (n + 1)].bitcast(FP4X4),
+                        lhsT_scale=w4_s[:, b, P * n : P * (n + 1)],
+                        rhs=h_codes[b, c][:, j0 : j0 + step].bitcast(FP8X4),
+                        rhs_scale=h_scales[b, c][:, j0 : j0 + step],
+                        start=(b == 0),
+                        stop=(b == 1),
+                    )
+            y_sb[n, c] = sb([P, w], F32, "y_sb%d%d" % (n, c))
+            nc.scalar.copy(y_sb[n, c][:], y[:, :w])
+
+        def scatter(n, c):
+            nc.vector.tensor_tensor(
+                windows[n][:].indirect(scatter_list[:, list_cols(c)]), y_sb[n, c][:], wgo_sb[c][:], ALU.mult
+            )
+
+        for c in range(3):
+            gather_words(0, c)
+        round_loadings(nc.scalar.copy, 0, 0, 0, P)
+        for c in range(3):
+            gather_scales(c)
+        quantise_loadings(0, 0, 0, PACK)
+        for c in range(3):
+            gather_words(1, c)
+        round_loadings(nc.scalar.copy, 1, 0, 0, P // 2)
+        round_loadings(nc.vector.tensor_copy, 1, 0, P // 2, P)
+        quantise_loadings(1, 0, 0, PACK)
+        nc.vector.tensor_scalar(minus_price[:], price_sb[:], -1.0, None, ALU.mult)
+        returns(0, 0)
+        round_loadings(nc.vector.tensor_copy, 0, 1, 0, P)
+        returns(0, 1)
+        quantise_loadings(0, 1, 0, PACK)
+        round_loadings(nc.vector.tensor_copy, 1, 1, 0, P // 2)
+        profit_on_vector(0, 0)
+        round_loadings(nc.vector.tensor_copy, 1, 1, P // 2, P)
+        for t in range(PACK):
+            quantise_loadings(1, 1, t, t + 1)
+        quantise_profit(0, 0)
+        returns(1, 0)
+        profit_on_vector(0, 1)
+        profit_on_vector(1, 0)
+        quantise_profit(1, 0)
+        returns(1, 1)
+        quantise_profit(0, 1)
+        for n in range(4):
+            portfolios(n, 0)
+        scatter(0, 0)
+        profit_on_scalar(1, 1)
+        scatter(1, 0)
+        quantise_profit(1, 1)
+        for n in range(4):
+            portfolios(n, 1)
+        returns(0, 2)
+        profit_on_scalar(0, 2)
+        returns(1, 2)
+        profit_on_scalar(1, 2)
+        scatter(2, 0)
+        scatter(3, 0)
+        scatter(0, 1)
+        quantise_profit(0, 2)
+        scatter(1, 1)
+        scatter(2, 1)
+        quantise_profit(1, 2)
+        for n in range(4):
+            portfolios(n, 2)
+        scatter(3, 1)
+        for n in range(4):
+            scatter(n, 2)
+            nc.sync.dma_start(out[P * n : P * (n + 1), :], windows[n][:])

@@ -18,8 +18,11 @@ ACT = mybir.ActivationFunctionType
 
 P = 128
 PACK = 4
-KP = P * PACK
-CHUNKS = [(0, 256), (256, 256), (512, 512)]
+PASS = P * PACK
+BANK = 512
+GROUP = 16
+CHUNK = 256
+QUADRANTS = 4
 
 
 def tile_list_scenario_profit_store_kernel(
@@ -28,136 +31,130 @@ def tile_list_scenario_profit_store_kernel(
     nc = tc.nc
     with ExitStack() as ctx:
         keep = ctx.enter_context(tc.tile_pool(name="keep", bufs=1))
-        psum_r = ctx.enter_context(tc.psum_pool(name="psum_r", bufs=5))
-        psum_y = ctx.enter_context(tc.psum_pool(name="psum_y", bufs=3))
+        psum = ctx.enter_context(tc.psum_pool(name="psum", bufs=1))
 
         def sb(shape, dtype, name):
             return keep.tile(shape, dtype, name=name, align_bytes=64)
 
-        gather_list = sb([P, S // 16], U16, "gather_list")
-        scatter_list = sb([P, S // 16], U16, "scatter_list")
+        gather_list = sb([P, S // GROUP], U16, "gather_list")
+        scatter_list = sb([P, S // GROUP], U16, "scatter_list")
         tab_w = [sb([P, T], I32, "tab_w%d" % a) for a in range(2)]
         tab_s = sb([P, T], U8, "tab_s")
-        raw = {(a, b): sb([P, PACK, KP], F32, "raw%d%d" % (a, b)) for a in range(2) for b in range(2)}
-        grouped = {ab: sb([P, PACK * KP], BF16, "grouped%d%d" % ab) for ab in raw}
-        l_codes = {ab: sb([P, KP], U32, "l_codes%d%d" % ab) for ab in raw}
-        l_scales = {ab: sb([P, KP], U8, "l_scales%d%d" % ab) for ab in raw}
+        v_codes = [sb([P, S], U32, "v_codes%d" % a) for a in range(2)]
+        v_scales = sb([P, S], U8, "v_scales")
+        blocks = [(a, b) for a in range(2) for b in range(2)]
+        l_rounded = {ab: sb([P, PACK * PASS], BF16, "l_rounded%d%d" % ab) for ab in blocks}
+        l_codes = {ab: sb([P, PASS], U32, "l_codes%d%d" % ab) for ab in blocks}
+        l_scales = {ab: sb([P, PASS], U8, "l_scales%d%d" % ab) for ab in blocks}
         drift_sb = sb([P, 2, PACK], F32, "drift_sb")
         price_sb = sb([P, 2, PACK], F32, "price_sb")
         minus_price = sb([P, 2, PACK], F32, "minus_price")
         w4_w = sb([P, 2, 2 * N], U8, "w4_w")
         w4_s = sb([P, 2, N], U8, "w4_s")
-        wgo_sb = [sb([P, w], F32, "wgo%d" % c) for c, (j0, w) in enumerate(CHUNKS)]
+        wgo_sb = sb([P, S], F32, "wgo_sb")
         windows = [sb([P, T2], F32, "window%d" % n) for n in range(N // P)]
-        v_codes = {(a, c): sb([P, w], U32, "v_codes%d%d" % (a, c)) for a in range(2) for c, (j0, w) in enumerate(CHUNKS)}
-        v_scales = [sb([P, w], U8, "v_scales%d" % c) for c, (j0, w) in enumerate(CHUNKS)]
-        warm = sb([P, 1], F32, "warm")
-        warm_out = sb([P, 1], F32, "warm_out")
-
-        def list_cols(c):
-            j0, w = CHUNKS[c]
-            return slice(j0 // 16, (j0 + w) // 16)
+        banks = [psum.tile([P, BANK], F32, name="bank%d" % i) for i in range(8)]
+        l_raw, growth, plane_words, h_rounded, h_codes, h_scales, y_bank, y_sb = ({} for i in range(8))
 
         nc.vector.memset(tab_s[:].bitcast(I32), 0)
-        nc.vector.memset(warm[:], 0.0)
-        nc.scalar.activation(warm_out[:], warm[:], ACT.Exp)
         nc.vector.memset(w4_s[:].rearrange("p b n -> p (b n)").bitcast(I32), 0)
-        for n in range(N // P):
-            nc.vector.memset(windows[n][:], 0.0)
+        for window in windows:
+            nc.vector.memset(window[:], 0.0)
 
-        def load_table_words(a):
+        def load_table(a):
             nc.sync.dma_start(tab_w[a][:], tab_words[a].rearrange("p t i -> p (t i)").bitcast(I32))
 
         def load_table_scales(a):
-            for q in range(4):
+            for q in range(QUADRANTS):
                 row = 32 * q + 4 * a
                 nc.sync.dma_start(
                     tab_s[row : row + 4, :].bitcast(I32), tab_scales[a, 4 * q : 4 * q + 4, :].bitcast(I32)
                 )
 
-        def load_loadings(a, b, c0, c1):
-            rows = load[KP * a : KP * (a + 1), KP * b + c0 : KP * b + c1]
-            nc.sync.dma_start(raw[a, b][:, :, c0:c1], rows.rearrange("(p j) c -> p j c", j=PACK))
+        def load_loadings(a, b, col0, col1):
+            l_raw[a, b, col0] = sb([P, PACK, col1 - col0], F32, "l_raw%d%d_%d" % (a, b, col0))
+            rows = load[PASS * a : PASS * (a + 1), PASS * b + col0 : PASS * b + col1]
+            nc.sync.dma_start(l_raw[a, b, col0][:], rows.rearrange("(p i) c -> p i c", i=PACK))
 
+        half = PASS // 2
+        load_table(0)
         nc.sync.dma_start(gather_list[:], offs)
-        load_table_words(0)
         load_table_scales(0)
-        load_loadings(0, 0, 0, KP)
+        load_loadings(0, 0, 0, PASS)
         load_table_scales(1)
-        load_table_words(1)
-        load_loadings(1, 0, 0, KP)
+        load_table(1)
         nc.sync.dma_start(drift_sb[:], drift.rearrange("(b p t) -> p b t", b=2, t=PACK))
         nc.sync.dma_start(price_sb[:], price.rearrange("(b p t) -> p b t", b=2, t=PACK))
-        load_loadings(0, 1, 0, KP)
-        load_loadings(1, 1, 0, KP // 2)
-        load_loadings(1, 1, KP // 2, KP)
-        nc.sync.dma_start(w4_w[:].bitcast(I32), w4_words.rearrange("b p c -> p b c").bitcast(I32))
-        for q in range(4):
+        for q in range(QUADRANTS):
             nc.sync.dma_start(
                 w4_s[32 * q : 32 * q + 4, :, :].bitcast(I32),
                 w4_scales[:, 4 * q : 4 * q + 4, :].rearrange("b r n -> r b n").bitcast(I32),
             )
+        load_loadings(1, 0, 0, PASS)
+        load_loadings(0, 1, 0, PASS)
+        load_loadings(1, 1, 0, half)
+        load_loadings(1, 1, half, PASS)
+        nc.sync.dma_start(w4_w[:].bitcast(I32), w4_words.rearrange("b p c -> p b c").bitcast(I32))
         nc.sync.dma_start(scatter_list[:], offs2)
-        for c, (j0, w) in enumerate(CHUNKS):
-            nc.sync.dma_start(wgo_sb[c][:], wgo[:, j0 : j0 + w])
+        nc.sync.dma_start(wgo_sb[:], wgo)
 
-        def gather_words(a, c):
-            nc.vector.tensor_copy(v_codes[a, c][:], tab_w[a][:].bitcast(U32).indirect(gather_list[:, list_cols(c)]))
+        def gather(dst, window, width):
+            for j0 in range(0, S, width):
+                entries = gather_list[:, j0 // GROUP : (j0 + width) // GROUP]
+                nc.vector.tensor_copy(dst[:, j0 : j0 + width], window.indirect(entries))
 
-        def gather_scales(c):
-            nc.vector.tensor_copy(v_scales[c][:], tab_s[:].indirect(gather_list[:, list_cols(c)]))
-
-        def round_loadings(copy, a, b, m0, m1):
+        def round_loadings(copy, a, b, col0):
+            piece = l_raw[a, b, col0]
+            m0, m1 = col0 // PACK, (col0 + piece.shape[2]) // PACK
             copy(
-                grouped[a, b][:].rearrange("p (t m j) -> p m j t", t=PACK, j=PACK)[:, m0:m1],
-                raw[a, b][:].rearrange("p j (m t) -> p m j t", t=PACK)[:, m0:m1],
+                l_rounded[a, b][:].rearrange("p (t m i) -> p m i t", t=PACK, i=PACK)[:, m0:m1],
+                piece[:].rearrange("p i (m t) -> p m i t", t=PACK),
             )
 
-        def quantise_loadings(a, b, t0, t1):
-            nc.vector.quantize_mx(
-                out=l_codes[a, b][:, P * t0 : P * t1].bitcast(FP8X4),
-                scales=l_scales[a, b][:, P * t0 : P * t1],
-                in_=grouped[a, b][:, KP * t0 : KP * t1],
-            )
+        def quantise_loadings(a, b, planes):
+            for t in range(0, PACK, planes):
+                nc.vector.quantize_mx(
+                    out=l_codes[a, b][:, P * t : P * (t + planes)].bitcast(FP8X4),
+                    scales=l_scales[a, b][:, P * t : P * (t + planes)],
+                    in_=l_rounded[a, b][:, PASS * t : PASS * (t + planes)],
+                )
 
-        growth = {}
-        h_grouped = {}
-        h_codes = {}
-        h_scales = {}
-
-        def returns(b, c):
-            w = CHUNKS[c][1]
-            growth[b, c] = sb([P, PACK, w], F32, "growth%d%d" % (b, c))
-            for t in range(PACK):
-                r = psum_r.tile([P, KP], F32, name="r")
-                for a in range(2):
+        def returns(b, c, first_bank, into=None):
+            cols = slice(CHUNK * c, CHUNK * (c + 1))
+            growth[b, c] = sb([P, PACK, CHUNK], F32, "growth%d%d" % (b, c)) if into is None else into
+            sums = banks[first_bank : first_bank + PACK]
+            for a in range(2):
+                for t in range(PACK):
                     nc.tensor.matmul_mx(
-                        out=r[:, :w],
+                        out=sums[t][:, :CHUNK],
                         lhsT=l_codes[a, b][:, P * t : P * (t + 1)].bitcast(FP8X4),
                         lhsT_scale=l_scales[a, b][:, P * t : P * (t + 1)],
-                        rhs=v_codes[a, c][:].bitcast(FP8X4),
-                        rhs_scale=v_scales[c][4 * a : P, :],
+                        rhs=v_codes[a][:, cols].bitcast(FP8X4),
+                        rhs_scale=v_scales[4 * a : P, cols],
                         start=(a == 0),
                         stop=(a == 1),
                     )
-                nc.scalar.activation(growth[b, c][:, t, :], r[:, :w], ACT.Exp, bias=drift_sb[:, b, t : t + 1])
+            for t in range(PACK):
+                nc.scalar.activation(
+                    growth[b, c][:, t, :], sums[t][:, :CHUNK], ACT.Exp, bias=drift_sb[:, b, t : t + 1]
+                )
 
-        def profit_on_vector(b, c):
-            w = CHUNKS[c][1]
-            h_grouped[b, c] = sb([P, w, PACK], BF16, "h_grouped%d%d" % (b, c))
+        def profit_on_vector(b, c, into=None):
+            h_rounded[b, c] = sb([P, CHUNK, PACK], BF16, "h_rounded%d%d" % (b, c)) if into is None else into
             nc.vector.scalar_tensor_tensor(
-                h_grouped[b, c][:],
+                h_rounded[b, c][:],
                 growth[b, c][:].rearrange("p t j -> p j t"),
                 -1.0,
-                price_sb[:, b, :].unsqueeze(1).to_broadcast([P, w, PACK]),
+                price_sb[:, b, :].unsqueeze(1).to_broadcast([P, CHUNK, PACK]),
                 ALU.add,
                 ALU.mult,
             )
 
         def profit_on_scalar(b, c):
-            w = CHUNKS[c][1]
-            planes = sb([P, PACK, w], BF16, "h_planes%d%d" % (b, c))
-            h_grouped[b, c] = sb([P, w, PACK], BF16, "h_grouped%d%d" % (b, c))
+            plane_words[b, c] = sb([P, 2, CHUNK], F32, "plane_words%d%d" % (b, c))
+            planes = plane_words[b, c][:].rearrange("p u j -> p (u j)").bitcast(BF16)
+            planes = planes.rearrange("p (t j) -> p t j", t=PACK)
+            h_rounded[b, c] = sb([P, CHUNK, PACK], BF16, "h_rounded%d%d" % (b, c))
             for t in range(PACK):
                 nc.scalar.activation(
                     planes[:, t, :],
@@ -167,95 +164,115 @@ def tile_list_scenario_profit_store_kernel(
                     scale=price_sb[:, b, t : t + 1],
                 )
             nc.scalar.copy(
-                h_grouped[b, c][:].rearrange("p (g i) t -> p g t i", i=4),
-                planes[:].rearrange("p t (g i) -> p g t i", i=4),
+                h_rounded[b, c][:].rearrange("p (g e) t -> p g t e", e=4),
+                planes.rearrange("p t (g e) -> p g t e", e=4),
             )
 
         def quantise_profit(b, c):
-            w = CHUNKS[c][1]
-            h_codes[b, c] = sb([P, w], U32, "h_codes%d%d" % (b, c))
-            h_scales[b, c] = sb([P, w], U8, "h_scales%d%d" % (b, c))
+            h_codes[b, c] = sb([P, CHUNK], U32, "h_codes%d%d" % (b, c))
+            h_scales[b, c] = sb([P, CHUNK], U8, "h_scales%d%d" % (b, c))
             nc.vector.quantize_mx(
                 out=h_codes[b, c][:].bitcast(FP8X4),
                 scales=h_scales[b, c][:],
-                in_=h_grouped[b, c][:].rearrange("p j t -> p (j t)"),
+                in_=h_rounded[b, c][:].rearrange("p j t -> p (j t)"),
             )
 
-        y_sb = {}
+        def portfolios(tiles, c, bank):
+            for place, n in enumerate(tiles):
+                for j0 in range(0, CHUNK, P):
+                    for b in range(2):
+                        nc.tensor.matmul_mx(
+                            out=bank[:, CHUNK * place + j0 : CHUNK * place + j0 + P],
+                            lhsT=w4_w[:, b, 2 * P * n : 2 * P * (n + 1)].bitcast(FP4X4),
+                            lhsT_scale=w4_s[:, b, P * n : P * (n + 1)],
+                            rhs=h_codes[b, c][:, j0 : j0 + P].bitcast(FP8X4),
+                            rhs_scale=h_scales[b, c][:, j0 : j0 + P],
+                            start=(b == 0),
+                            stop=(b == 1),
+                        )
+            y_bank[tiles, c] = bank
 
-        def portfolios(n, c):
-            w = CHUNKS[c][1]
-            step = KP if w == KP else P
-            y = psum_y.tile([P, KP], F32, name="y")
-            for j0 in range(0, w, step):
-                for b in range(2):
-                    nc.tensor.matmul_mx(
-                        out=y[:, j0 : j0 + step],
-                        lhsT=w4_w[:, b, 2 * P * n : 2 * P * (n + 1)].bitcast(FP4X4),
-                        lhsT_scale=w4_s[:, b, P * n : P * (n + 1)],
-                        rhs=h_codes[b, c][:, j0 : j0 + step].bitcast(FP8X4),
-                        rhs_scale=h_scales[b, c][:, j0 : j0 + step],
-                        start=(b == 0),
-                        stop=(b == 1),
-                    )
-            y_sb[n, c] = sb([P, w], F32, "y_sb%d%d" % (n, c))
-            nc.scalar.copy(y_sb[n, c][:], y[:, :w])
+        def evacuate(tiles, c, into=None):
+            dst = sb([P, len(tiles), CHUNK], F32, "y_sb%d%d" % (tiles[0], c)) if into is None else into
+            nc.scalar.copy(dst[:].rearrange("p u j -> p (u j)"), y_bank[tiles, c][:, : CHUNK * len(tiles)])
+            for place, n in enumerate(tiles):
+                y_sb[n, c] = dst[:, place, :]
 
         def scatter(n, c):
+            entries = scatter_list[:, CHUNK * c // GROUP : CHUNK * (c + 1) // GROUP]
             nc.vector.tensor_tensor(
-                windows[n][:].indirect(scatter_list[:, list_cols(c)]), y_sb[n, c][:], wgo_sb[c][:], ALU.mult
+                windows[n][:].indirect(entries), y_sb[n, c], wgo_sb[:, CHUNK * c : CHUNK * (c + 1)], ALU.mult
             )
 
-        for c in range(3):
-            gather_words(0, c)
-        round_loadings(nc.scalar.copy, 0, 0, 0, P)
-        for c in range(3):
-            gather_scales(c)
-        quantise_loadings(0, 0, 0, PACK)
-        for c in range(3):
-            gather_words(1, c)
-        round_loadings(nc.scalar.copy, 1, 0, 0, P // 2)
-        round_loadings(nc.vector.tensor_copy, 1, 0, P // 2, P)
-        quantise_loadings(1, 0, 0, PACK)
-        nc.vector.tensor_scalar(minus_price[:], price_sb[:], -1.0, None, ALU.mult)
-        returns(0, 0)
-        round_loadings(nc.vector.tensor_copy, 0, 1, 0, P)
-        returns(0, 1)
-        quantise_loadings(0, 1, 0, PACK)
-        round_loadings(nc.vector.tensor_copy, 1, 1, 0, P // 2)
-        profit_on_vector(0, 0)
-        round_loadings(nc.vector.tensor_copy, 1, 1, P // 2, P)
-        for t in range(PACK):
-            quantise_loadings(1, 1, t, t + 1)
-        quantise_profit(0, 0)
-        returns(1, 0)
-        profit_on_vector(0, 1)
-        profit_on_vector(1, 0)
-        quantise_profit(1, 0)
-        returns(1, 1)
-        quantise_profit(0, 1)
-        for n in range(4):
-            portfolios(n, 0)
-        scatter(0, 0)
-        profit_on_scalar(1, 1)
-        scatter(1, 0)
-        quantise_profit(1, 1)
-        for n in range(4):
-            portfolios(n, 1)
-        returns(0, 2)
-        profit_on_scalar(0, 2)
-        returns(1, 2)
-        profit_on_scalar(1, 2)
-        scatter(2, 0)
-        scatter(3, 0)
-        scatter(0, 1)
-        quantise_profit(0, 2)
-        scatter(1, 1)
-        scatter(2, 1)
-        quantise_profit(1, 2)
-        for n in range(4):
-            portfolios(n, 2)
-        scatter(3, 1)
-        for n in range(4):
-            scatter(n, 2)
+        def store(n):
             nc.sync.dma_start(out[P * n : P * (n + 1), :], windows[n][:])
+
+        gather(v_codes[0], tab_w[0][:].bitcast(U32), S)
+        round_loadings(nc.scalar.copy, 0, 0, 0)
+        gather(v_scales, tab_s[:], S)
+        gather(v_codes[1], tab_w[1][:].bitcast(U32), S)
+        nc.scalar.activation(minus_price[:], price_sb[:], ACT.Identity, scale=-1.0)
+        round_loadings(nc.scalar.copy, 1, 0, 0)
+        round_loadings(nc.scalar.copy, 0, 1, 0)
+        round_loadings(nc.vector.tensor_copy, 1, 1, 0)
+        round_loadings(nc.vector.tensor_copy, 1, 1, half)
+        quantise_loadings(1, 0, 4)
+        quantise_loadings(0, 0, PACK)
+        quantise_loadings(0, 1, 2)
+        returns(0, 0, 0)
+        quantise_loadings(1, 1, 2)
+
+        profit_on_vector(0, 0, l_rounded[1, 1][:, 2 * PASS :].rearrange("p (j t) -> p j t", t=PACK))
+        returns(1, 0, 0)
+        returns(1, 1, 0)
+        profit_on_vector(1, 0)
+        quantise_profit(0, 0)
+        quantise_profit(1, 0)
+        profit_on_scalar(1, 1)
+        returns(0, 1, 4)
+        portfolios((0,), 0, banks[2])
+        portfolios((1,), 0, banks[3])
+        portfolios((2, 3), 0, banks[6])
+        evacuate((0,), 0)
+        evacuate((1,), 0)
+        quantise_profit(1, 1)
+        profit_on_vector(0, 1, h_rounded[1, 0])
+        scatter(0, 0)
+        scatter(1, 0)
+        quantise_profit(0, 1)
+
+        for c in range(2):
+            evacuate((2, 3), c, plane_words[1, c + 1])
+            returns(0, c + 2, 0)
+            returns(1, c + 2, 4)
+            portfolios((0, 1), c + 1, banks[7])
+            if c == 0:
+                portfolios((2, 3), 1, banks[6])
+            else:
+                portfolios((2,), 2, banks[6])
+                portfolios((3,), 2, banks[5])
+            scatter(2, c)
+            scatter(3, c)
+            profit_on_scalar(0, c + 2)
+            evacuate((0, 1), c + 1, plane_words[0, 2] if c == 0 else growth[0, 3][:, 2:4, :])
+            profit_on_scalar(1, c + 2)
+            quantise_profit(0, c + 2)
+            scatter(0, c + 1)
+            scatter(1, c + 1)
+            quantise_profit(1, c + 2)
+
+        evacuate((2,), 2, plane_words[1, 3][:, 0:1, :])
+        portfolios((0,), 3, banks[0])
+        portfolios((1, 2), 3, banks[1])
+        portfolios((3,), 3, banks[2])
+        evacuate((0,), 3)
+        evacuate((1, 2), 3)
+        scatter(2, 2)
+        for n in range(3):
+            scatter(n, 3)
+            store(n)
+        evacuate((3,), 3, y_sb[0, 3].unsqueeze(1))
+        evacuate((3,), 2, y_sb[1, 3].unsqueeze(1))
+        scatter(3, 3)
+        scatter(3, 2)
+        store(3)

@@ -33,18 +33,19 @@ def tile_list_scenario_profit_store_kernel(
         keep = ctx.enter_context(tc.tile_pool(name="keep", bufs=1))
         psum = ctx.enter_context(tc.psum_pool(name="psum", bufs=1))
 
-        def sb(shape, dtype, name):
-            return keep.tile(shape, dtype, name=name, align_bytes=64)
+        def sb(shape, dtype, name, over=None):
+            return keep.tile(shape, dtype, name=name, tag=over or name, align_bytes=64)
 
         gather_list = sb([P, S // GROUP], U16, "gather_list")
         scatter_list = sb([P, S // GROUP], U16, "scatter_list")
         tab_w = [sb([P, T], I32, "tab_w%d" % a) for a in range(2)]
         tab_s = sb([P, T], U8, "tab_s")
-        v_codes = [sb([P, S], U32, "v_codes%d" % a) for a in range(2)]
+        v_first = sb([P, S], U32, "v_first")
+        v_second = [sb([P, S - CHUNK], U32, "v_second0")]
         v_scales = sb([P, S], U8, "v_scales")
         blocks = [(a, b) for a in range(2) for b in range(2)]
-        l_rounded = {ab: sb([P, PACK * PASS], BF16, "l_rounded%d%d" % ab) for ab in blocks}
-        l_codes = {ab: sb([P, PASS], U32, "l_codes%d%d" % ab) for ab in blocks}
+        l_rounded = {ab: sb([P, PACK * PASS], BF16, "l_rounded%d%d" % ab) for ab in blocks[:3]}
+        l_codes = {ab: sb([P, PASS], U32, "l_codes%d%d" % ab) for ab in blocks[1:]}
         l_scales = {ab: sb([P, PASS], U8, "l_scales%d%d" % ab) for ab in blocks}
         drift_sb = sb([P, 2, PACK], F32, "drift_sb")
         price_sb = sb([P, 2, PACK], F32, "price_sb")
@@ -54,7 +55,7 @@ def tile_list_scenario_profit_store_kernel(
         wgo_sb = sb([P, S], F32, "wgo_sb")
         windows = [sb([P, T2], F32, "window%d" % n) for n in range(N // P)]
         banks = [psum.tile([P, BANK], F32, name="bank%d" % i) for i in range(8)]
-        l_raw, growth, plane_words, h_rounded, h_codes, h_scales, y_bank, y_sb = ({} for i in range(8))
+        l_raw, sums, growth, planes, h_rounded, h_codes, h_scales, y_sums = ({} for i in range(8))
 
         nc.vector.memset(tab_s[:].bitcast(I32), 0)
         nc.vector.memset(w4_s[:].rearrange("p b n -> p (b n)").bitcast(I32), 0)
@@ -82,197 +83,254 @@ def tile_list_scenario_profit_store_kernel(
         load_table_scales(0)
         load_loadings(0, 0, 0, PASS)
         load_table_scales(1)
-        load_table(1)
+        load_loadings(1, 0, 0, PASS)
         nc.sync.dma_start(drift_sb[:], drift.rearrange("(b p t) -> p b t", b=2, t=PACK))
         nc.sync.dma_start(price_sb[:], price.rearrange("(b p t) -> p b t", b=2, t=PACK))
+        load_table(1)
         for q in range(QUADRANTS):
             nc.sync.dma_start(
                 w4_s[32 * q : 32 * q + 4, :, :].bitcast(I32),
                 w4_scales[:, 4 * q : 4 * q + 4, :].rearrange("b r n -> r b n").bitcast(I32),
             )
-        load_loadings(1, 0, 0, PASS)
+        nc.sync.dma_start(scatter_list[:], offs2)
         load_loadings(0, 1, 0, PASS)
         load_loadings(1, 1, 0, half)
         load_loadings(1, 1, half, PASS)
         nc.sync.dma_start(w4_w[:].bitcast(I32), w4_words.rearrange("b p c -> p b c").bitcast(I32))
-        nc.sync.dma_start(scatter_list[:], offs2)
         nc.sync.dma_start(wgo_sb[:], wgo)
 
-        def gather(dst, window, width):
-            for j0 in range(0, S, width):
-                entries = gather_list[:, j0 // GROUP : (j0 + width) // GROUP]
-                nc.vector.tensor_copy(dst[:, j0 : j0 + width], window.indirect(entries))
+        def gather(dst, window, j0, j1):
+            entries = gather_list[:, j0 // GROUP : j1 // GROUP]
+            nc.vector.tensor_copy(dst, window.indirect(entries))
 
-        def round_loadings(copy, a, b, col0):
+        def round_loadings(copy, a, b, col0, t0=0, t1=PACK):
             piece = l_raw[a, b, col0]
             m0, m1 = col0 // PACK, (col0 + piece.shape[2]) // PACK
             copy(
-                l_rounded[a, b][:].rearrange("p (t m i) -> p m i t", t=PACK, i=PACK)[:, m0:m1],
-                piece[:].rearrange("p i (m t) -> p m i t", t=PACK),
+                l_rounded[a, b][:].rearrange("p (t m i) -> p m i t", t=PACK, i=PACK)[:, m0:m1, :, t0:t1],
+                piece[:].rearrange("p i (m t) -> p m i t", t=PACK)[:, :, :, t0:t1],
             )
 
-        def quantise_loadings(a, b, planes):
-            for t in range(0, PACK, planes):
+        def quantise_loadings(a, b, planes, t0=0, t1=PACK):
+            for t in range(t0, t1, planes):
                 nc.vector.quantize_mx(
                     out=l_codes[a, b][:, P * t : P * (t + planes)].bitcast(FP8X4),
                     scales=l_scales[a, b][:, P * t : P * (t + planes)],
                     in_=l_rounded[a, b][:, PASS * t : PASS * (t + planes)],
                 )
 
-        def returns(b, c, first_bank, into=None):
+        def v_codes(a, c):
+            if a == 0:
+                return v_first[:, CHUNK * c : CHUNK * (c + 1)]
+            return v_second[c // 3][:, CHUNK * (c % 3) : CHUNK * (c % 3 + 1)]
+
+        def log_returns(b, c, used):
             cols = slice(CHUNK * c, CHUNK * (c + 1))
-            growth[b, c] = sb([P, PACK, CHUNK], F32, "growth%d%d" % (b, c)) if into is None else into
-            sums = banks[first_bank : first_bank + PACK]
-            for a in range(2):
-                for t in range(PACK):
+            share = PACK // len(used)
+            for t in range(PACK):
+                place = CHUNK * (t % share)
+                sums[b, c, t] = banks[used[t // share]][:, place : place + CHUNK]
+                for a in range(2):
                     nc.tensor.matmul_mx(
-                        out=sums[t][:, :CHUNK],
+                        out=sums[b, c, t],
                         lhsT=l_codes[a, b][:, P * t : P * (t + 1)].bitcast(FP8X4),
                         lhsT_scale=l_scales[a, b][:, P * t : P * (t + 1)],
-                        rhs=v_codes[a][:, cols].bitcast(FP8X4),
+                        rhs=v_codes(a, c).bitcast(FP8X4),
                         rhs_scale=v_scales[4 * a : P, cols],
                         start=(a == 0),
                         stop=(a == 1),
                     )
-            for t in range(PACK):
+
+        def exponentials(b, c, j0=0, j1=CHUNK, over=None, t0=0, t1=PACK):
+            if t0 == 0:
+                growth[b, c, j0] = sb([P, PACK, j1 - j0], F32, "growth%d%d_%d" % (b, c, j0), over)
+            for t in range(t0, t1):
                 nc.scalar.activation(
-                    growth[b, c][:, t, :], sums[t][:, :CHUNK], ACT.Exp, bias=drift_sb[:, b, t : t + 1]
+                    growth[b, c, j0][:, t, :], sums[b, c, t][:, j0:j1], ACT.Exp, bias=drift_sb[:, b, t : t + 1]
                 )
 
-        def profit_on_vector(b, c, into=None):
-            h_rounded[b, c] = sb([P, CHUNK, PACK], BF16, "h_rounded%d%d" % (b, c)) if into is None else into
+        def profit_on_vector(b, c, j0=0):
+            width = growth[b, c, j0].shape[2]
             nc.vector.scalar_tensor_tensor(
-                h_rounded[b, c][:],
-                growth[b, c][:].rearrange("p t j -> p j t"),
+                h_rounded[b, c, j0].rearrange("p (j t) -> p j t", t=PACK),
+                growth[b, c, j0][:].rearrange("p t j -> p j t"),
                 -1.0,
-                price_sb[:, b, :].unsqueeze(1).to_broadcast([P, CHUNK, PACK]),
+                price_sb[:, b, :].unsqueeze(1).to_broadcast([P, width, PACK]),
                 ALU.add,
                 ALU.mult,
             )
 
-        def profit_on_scalar(b, c):
-            plane_words[b, c] = sb([P, 2, CHUNK], F32, "plane_words%d%d" % (b, c))
-            planes = plane_words[b, c][:].rearrange("p u j -> p (u j)").bitcast(BF16)
-            planes = planes.rearrange("p (t j) -> p t j", t=PACK)
-            h_rounded[b, c] = sb([P, CHUNK, PACK], BF16, "h_rounded%d%d" % (b, c))
+        def profit_planes(b, c):
+            planes[b, c] = sb([P, PACK, CHUNK], BF16, "planes%d%d" % (b, c))
             for t in range(PACK):
                 nc.scalar.activation(
-                    planes[:, t, :],
-                    growth[b, c][:, t, :],
+                    planes[b, c][:, t, :],
+                    growth[b, c, 0][:, t, :],
                     ACT.Identity,
                     bias=minus_price[:, b, t : t + 1],
                     scale=price_sb[:, b, t : t + 1],
                 )
+
+        def interleave(b, c):
+            h_rounded[b, c, 0] = sb([P, CHUNK * PACK], BF16, "h_rounded%d%d" % (b, c))[:]
             nc.scalar.copy(
-                h_rounded[b, c][:].rearrange("p (g e) t -> p g t e", e=4),
-                planes.rearrange("p t (g e) -> p g t e", e=4),
+                h_rounded[b, c, 0].rearrange("p (g e t) -> p g t e", e=4, t=PACK),
+                planes[b, c][:].rearrange("p t (g e) -> p g t e", e=4),
             )
 
-        def quantise_profit(b, c):
-            h_codes[b, c] = sb([P, CHUNK], U32, "h_codes%d%d" % (b, c))
-            h_scales[b, c] = sb([P, CHUNK], U8, "h_scales%d%d" % (b, c))
+        def quantise_profit(b, c, j0=0, j1=CHUNK):
             nc.vector.quantize_mx(
-                out=h_codes[b, c][:].bitcast(FP8X4),
-                scales=h_scales[b, c][:],
-                in_=h_rounded[b, c][:].rearrange("p j t -> p (j t)"),
+                out=h_codes[b, c][:, j0:j1].bitcast(FP8X4),
+                scales=h_scales[b, c][:, j0:j1],
+                in_=h_rounded[b, c, j0],
             )
 
-        def portfolios(tiles, c, bank):
-            for place, n in enumerate(tiles):
+        def portfolios(n, c, bank, place=0):
+            y_sums[n, c] = banks[bank][:, CHUNK * place : CHUNK * (place + 1)]
+            for b in range(2):
                 for j0 in range(0, CHUNK, P):
-                    for b in range(2):
-                        nc.tensor.matmul_mx(
-                            out=bank[:, CHUNK * place + j0 : CHUNK * place + j0 + P],
-                            lhsT=w4_w[:, b, 2 * P * n : 2 * P * (n + 1)].bitcast(FP4X4),
-                            lhsT_scale=w4_s[:, b, P * n : P * (n + 1)],
-                            rhs=h_codes[b, c][:, j0 : j0 + P].bitcast(FP8X4),
-                            rhs_scale=h_scales[b, c][:, j0 : j0 + P],
-                            start=(b == 0),
-                            stop=(b == 1),
-                        )
-            y_bank[tiles, c] = bank
+                    nc.tensor.matmul_mx(
+                        out=y_sums[n, c][:, j0 : j0 + P],
+                        lhsT=w4_w[:, b, 2 * P * n : 2 * P * (n + 1)].bitcast(FP4X4),
+                        lhsT_scale=w4_s[:, b, P * n : P * (n + 1)],
+                        rhs=h_codes[b, c][:, j0 : j0 + P].bitcast(FP8X4),
+                        rhs_scale=h_scales[b, c][:, j0 : j0 + P],
+                        start=(b == 0 and j0 == 0),
+                        stop=(b == 1 and j0 == CHUNK - P),
+                    )
 
-        def evacuate(tiles, c, into=None):
-            dst = sb([P, len(tiles), CHUNK], F32, "y_sb%d%d" % (tiles[0], c)) if into is None else into
-            nc.scalar.copy(dst[:].rearrange("p u j -> p (u j)"), y_bank[tiles, c][:, : CHUNK * len(tiles)])
-            for place, n in enumerate(tiles):
-                y_sb[n, c] = dst[:, place, :]
+        def portfolios_late(n, bank):
+            y_sums[n, 2] = banks[bank][:]
+            for b in range(2):
+                nc.tensor.matmul_mx(
+                    out=y_sums[n, 2],
+                    lhsT=w4_w[:, b, 2 * P * n : 2 * P * (n + 1)].bitcast(FP4X4),
+                    lhsT_scale=w4_s[:, b, P * n : P * (n + 1)],
+                    rhs=late_codes[b][:].bitcast(FP8X4),
+                    rhs_scale=late_scales[b][:],
+                    start=(b == 0),
+                    stop=(b == 1),
+                )
 
-        def scatter(n, c):
-            entries = scatter_list[:, CHUNK * c // GROUP : CHUNK * (c + 1) // GROUP]
-            nc.vector.tensor_tensor(
-                windows[n][:].indirect(entries), y_sb[n, c], wgo_sb[:, CHUNK * c : CHUNK * (c + 1)], ALU.mult
-            )
+        def place_results(n, c, over=None):
+            width = y_sums[n, c].shape[1]
+            y_sb = sb([P, width], F32, "y_sb%d%d" % (n, c), over)
+            nc.scalar.copy(y_sb[:], y_sums[n, c])
+            j0 = CHUNK * c
+            entries = scatter_list[:, j0 // GROUP : (j0 + width) // GROUP]
+            nc.vector.tensor_tensor(windows[n][:].indirect(entries), y_sb[:], wgo_sb[:, j0 : j0 + width], ALU.mult)
 
         def store(n):
             nc.sync.dma_start(out[P * n : P * (n + 1), :], windows[n][:])
 
-        gather(v_codes[0], tab_w[0][:].bitcast(U32), S)
+        late_codes = [sb([P, 2 * CHUNK], U32, "late_codes%d" % b) for b in range(2)]
+        late_scales = [sb([P, 2 * CHUNK], U8, "late_scales%d" % b) for b in range(2)]
+        for b in range(2):
+            for c in range(2):
+                h_scales[b, c] = sb([P, CHUNK], U8, "h_scales%d%d" % (b, c))[:]
+                h_scales[b, c + 2] = late_scales[b][:, CHUNK * c : CHUNK * (c + 1)]
+                h_codes[b, c + 2] = late_codes[b][:, CHUNK * c : CHUNK * (c + 1)]
+        for bc in ((0, 0), (1, 0), (1, 1)):
+            h_codes[bc] = sb([P, CHUNK], U32, "h_codes%d%d" % bc)[:]
+
+        gather(v_first[:], tab_w[0][:].bitcast(U32), 0, S)
         round_loadings(nc.scalar.copy, 0, 0, 0)
-        gather(v_scales, tab_s[:], S)
-        gather(v_codes[1], tab_w[1][:].bitcast(U32), S)
-        nc.scalar.activation(minus_price[:], price_sb[:], ACT.Identity, scale=-1.0)
-        round_loadings(nc.scalar.copy, 1, 0, 0)
-        round_loadings(nc.scalar.copy, 0, 1, 0)
-        round_loadings(nc.vector.tensor_copy, 1, 1, 0)
-        round_loadings(nc.vector.tensor_copy, 1, 1, half)
-        quantise_loadings(1, 0, 4)
+        gather(v_scales[:], tab_s[:], 0, S)
+        l_codes[0, 0] = sb([P, PASS], U32, "l_codes00", over="tab_s")
         quantise_loadings(0, 0, PACK)
-        quantise_loadings(0, 1, 2)
-        returns(0, 0, 0)
-        quantise_loadings(1, 1, 2)
+        round_loadings(nc.scalar.copy, 1, 0, 0, 0, 2)
+        round_loadings(nc.vector.tensor_copy, 1, 0, 0, 2, 4)
+        nc.scalar.activation(minus_price[:], price_sb[:], ACT.Identity, scale=-1.0)
+        quantise_loadings(1, 0, 2)
+        gather(v_codes(1, 0), tab_w[1][:].bitcast(U32), 0, CHUNK)
+        gather(v_second[0][:, CHUNK:], tab_w[1][:].bitcast(U32), CHUNK, S - CHUNK)
+        log_returns(0, 0, (0, 1, 2, 3))
+        exponentials(0, 0)
+        log_returns(0, 1, (4, 5))
+        exponentials(0, 1)
+        profit_planes(0, 1)
+        interleave(0, 1)
+        log_returns(0, 2, (6, 7))
+        round_loadings(nc.vector.tensor_copy, 0, 1, 0, 0, 2)
+        round_loadings(nc.vector.tensor_copy, 0, 1, 0, 2, 4)
+        quantise_loadings(0, 1, 2, 0, 2)
+        l_rounded[1, 1] = sb([P, PACK * PASS], BF16, "l_rounded11", over="l_raw01_0")
+        round_loadings(nc.vector.tensor_copy, 1, 1, 0)
+        quantise_loadings(0, 1, 2, 2, 4)
+        round_loadings(nc.vector.tensor_copy, 1, 1, half)
+        quantise_loadings(1, 1, 1)
 
-        profit_on_vector(0, 0, l_rounded[1, 1][:, 2 * PASS :].rearrange("p (j t) -> p j t", t=PACK))
-        returns(1, 0, 0)
-        returns(1, 1, 0)
-        profit_on_vector(1, 0)
+        h_rounded[0, 0, 0] = l_rounded[1, 1][:, PASS : 3 * PASS]
+        profit_on_vector(0, 0)
         quantise_profit(0, 0)
-        quantise_profit(1, 0)
-        profit_on_scalar(1, 1)
-        returns(0, 1, 4)
-        portfolios((0,), 0, banks[2])
-        portfolios((1,), 0, banks[3])
-        portfolios((2, 3), 0, banks[6])
-        evacuate((0,), 0)
-        evacuate((1,), 0)
-        quantise_profit(1, 1)
-        profit_on_vector(0, 1, h_rounded[1, 0])
-        scatter(0, 0)
-        scatter(1, 0)
+        log_returns(1, 0, (0, 1, 2, 3))
+        exponentials(1, 0, 0, P)
+        exponentials(1, 0, P, CHUNK)
+        for j0 in (0, P):
+            h_rounded[1, 0, j0] = sb([P, P * PACK], BF16, "h_rounded10_%d" % j0)[:]
+        profit_on_vector(1, 0, 0)
+        profit_on_vector(1, 0, P)
+        quantise_profit(1, 0, 0, P)
+        quantise_profit(1, 0, P, CHUNK)
+        h_codes[0, 1] = sb([P, CHUNK], U32, "h_codes01", over="h_rounded10_0")[:]
         quantise_profit(0, 1)
-
-        for c in range(2):
-            evacuate((2, 3), c, plane_words[1, c + 1])
-            returns(0, c + 2, 0)
-            returns(1, c + 2, 4)
-            portfolios((0, 1), c + 1, banks[7])
-            if c == 0:
-                portfolios((2, 3), 1, banks[6])
-            else:
-                portfolios((2,), 2, banks[6])
-                portfolios((3,), 2, banks[5])
-            scatter(2, c)
-            scatter(3, c)
-            profit_on_scalar(0, c + 2)
-            evacuate((0, 1), c + 1, plane_words[0, 2] if c == 0 else growth[0, 3][:, 2:4, :])
-            profit_on_scalar(1, c + 2)
-            quantise_profit(0, c + 2)
-            scatter(0, c + 1)
-            scatter(1, c + 1)
-            quantise_profit(1, c + 2)
-
-        evacuate((2,), 2, plane_words[1, 3][:, 0:1, :])
-        portfolios((0,), 3, banks[0])
-        portfolios((1, 2), 3, banks[1])
-        portfolios((3,), 3, banks[2])
-        evacuate((0,), 3)
-        evacuate((1, 2), 3)
-        scatter(2, 2)
-        for n in range(3):
-            scatter(n, 3)
+        v_second.append(sb([P, CHUNK], U32, "v_second1", over="h_rounded10_128"))
+        gather(v_second[1][:], tab_w[1][:].bitcast(U32), S - CHUNK, S)
+        log_returns(1, 1, (4, 5))
+        exponentials(1, 1)
+        portfolios(0, 0, 2)
+        portfolios(1, 0, 3)
+        portfolios(2, 0, 0)
+        portfolios(3, 0, 0, 1)
+        profit_planes(1, 1)
+        place_results(0, 0)
+        exponentials(0, 2, over="growth11_0", t1=2)
+        place_results(1, 0)
+        exponentials(0, 2, t0=2)
+        log_returns(1, 2, (2, 3))
+        log_returns(0, 3, (6, 7))
+        interleave(1, 1)
+        quantise_profit(1, 1)
+        portfolios(0, 1, 1)
+        portfolios(1, 1, 1, 1)
+        portfolios(2, 1, 4)
+        portfolios(3, 1, 4, 1)
+        place_results(2, 0, over="planes11")
+        profit_planes(0, 2)
+        place_results(3, 0)
+        interleave(0, 2)
+        quantise_profit(0, 2)
+        exponentials(1, 2)
+        log_returns(1, 3, (2, 3))
+        place_results(0, 1)
+        profit_planes(1, 2)
+        place_results(1, 1)
+        interleave(1, 2)
+        quantise_profit(1, 2)
+        portfolios(0, 2, 5)
+        portfolios(1, 2, 5, 1)
+        portfolios(2, 2, 0)
+        place_results(2, 1, over="planes12")
+        exponentials(0, 3)
+        profit_planes(0, 3)
+        place_results(3, 1)
+        interleave(0, 3)
+        quantise_profit(0, 3)
+        place_results(0, 2, over="planes03")
+        exponentials(1, 3)
+        profit_planes(1, 3)
+        place_results(1, 2)
+        interleave(1, 3)
+        quantise_profit(1, 3)
+        portfolios(0, 3, 1)
+        portfolios(1, 3, 4)
+        portfolios(2, 3, 4, 1)
+        place_results(2, 2, over="planes13")
+        place_results(0, 3)
+        store(0)
+        for n in (1, 2):
+            place_results(n, 3)
             store(n)
-        evacuate((3,), 3, y_sb[0, 3].unsqueeze(1))
-        evacuate((3,), 2, y_sb[1, 3].unsqueeze(1))
-        scatter(3, 3)
-        scatter(3, 2)
+        portfolios_late(3, 4)
+        place_results(3, 2)
         store(3)

@@ -55,7 +55,7 @@ def tile_list_scenario_profit_store_kernel(
         wgo_sb = sb([P, S], F32, "wgo_sb")
         windows = [sb([P, T2], F32, "window%d" % n) for n in range(N // P)]
         banks = [psum.tile([P, BANK], F32, name="bank%d" % i) for i in range(8)]
-        l_raw, sums, growth, planes, h_rounded, h_codes, h_scales, y_sums = ({} for i in range(8))
+        l_raw, sums, growth, planes, h_rounded, h_codes, h_scales, y_sums, plane = ({} for i in range(9))
 
         nc.vector.memset(tab_s[:].bitcast(I32), 0)
         nc.vector.memset(w4_s[:].rearrange("p b n -> p (b n)").bitcast(I32), 0)
@@ -77,27 +77,29 @@ def tile_list_scenario_profit_store_kernel(
             rows = load[PASS * a : PASS * (a + 1), PASS * b + col0 : PASS * b + col1]
             nc.sync.dma_start(l_raw[a, b, col0][:], rows.rearrange("(p i) c -> p i c", i=PACK))
 
-        half = PASS // 2
+        half, last = PASS // 2, PASS - P
         load_table(0)
         nc.sync.dma_start(gather_list[:], offs)
         load_table_scales(0)
         load_loadings(0, 0, 0, PASS)
         load_table_scales(1)
         load_loadings(1, 0, 0, PASS)
-        nc.sync.dma_start(drift_sb[:], drift.rearrange("(b p t) -> p b t", b=2, t=PACK))
-        nc.sync.dma_start(price_sb[:], price.rearrange("(b p t) -> p b t", b=2, t=PACK))
         load_table(1)
+        nc.sync.dma_start(drift_sb[:], drift.rearrange("(b p t) -> p b t", b=2, t=PACK))
+        load_loadings(0, 1, 0, half)
+        nc.sync.dma_start(price_sb[:], price.rearrange("(b p t) -> p b t", b=2, t=PACK))
+        load_loadings(0, 1, half, PASS)
+        load_loadings(1, 1, 0, half)
+        load_loadings(1, 1, half, last)
+        load_loadings(1, 1, last, PASS)
+        nc.sync.dma_start(wgo_sb[:], wgo)
+        nc.sync.dma_start(scatter_list[:], offs2)
+        nc.sync.dma_start(w4_w[:].bitcast(I32), w4_words.rearrange("b p c -> p b c").bitcast(I32))
         for q in range(QUADRANTS):
             nc.sync.dma_start(
                 w4_s[32 * q : 32 * q + 4, :, :].bitcast(I32),
                 w4_scales[:, 4 * q : 4 * q + 4, :].rearrange("b r n -> r b n").bitcast(I32),
             )
-        nc.sync.dma_start(scatter_list[:], offs2)
-        load_loadings(0, 1, 0, PASS)
-        load_loadings(1, 1, 0, half)
-        load_loadings(1, 1, half, PASS)
-        nc.sync.dma_start(w4_w[:].bitcast(I32), w4_words.rearrange("b p c -> p b c").bitcast(I32))
-        nc.sync.dma_start(wgo_sb[:], wgo)
 
         def gather(dst, window, j0, j1):
             entries = gather_list[:, j0 // GROUP : j1 // GROUP]
@@ -124,12 +126,12 @@ def tile_list_scenario_profit_store_kernel(
                 return v_first[:, CHUNK * c : CHUNK * (c + 1)]
             return v_second[c // 3][:, CHUNK * (c % 3) : CHUNK * (c % 3 + 1)]
 
-        def log_returns(b, c, used):
+        def log_returns(b, c, used, order=range(PACK)):
             cols = slice(CHUNK * c, CHUNK * (c + 1))
             share = PACK // len(used)
-            for t in range(PACK):
-                place = CHUNK * (t % share)
-                sums[b, c, t] = banks[used[t // share]][:, place : place + CHUNK]
+            for k, t in enumerate(order):
+                place = CHUNK * (k % share)
+                sums[b, c, t] = banks[used[k // share]][:, place : place + CHUNK]
                 for a in range(2):
                     nc.tensor.matmul_mx(
                         out=sums[b, c, t],
@@ -142,11 +144,11 @@ def tile_list_scenario_profit_store_kernel(
                     )
 
         def exponentials(b, c, j0=0, j1=CHUNK, over=None, t0=0, t1=PACK):
-            if t0 == 0:
-                growth[b, c, j0] = sb([P, PACK, j1 - j0], F32, "growth%d%d_%d" % (b, c, j0), over)
+            growth[b, c, j0] = sb([P, t1 - t0, j1 - j0], F32, "growth%d%d_%d_%d" % (b, c, j0, t0), over)
             for t in range(t0, t1):
+                plane[b, c, t] = growth[b, c, j0][:, t - t0, :]
                 nc.scalar.activation(
-                    growth[b, c, j0][:, t, :], sums[b, c, t][:, j0:j1], ACT.Exp, bias=drift_sb[:, b, t : t + 1]
+                    plane[b, c, t], sums[b, c, t][:, j0:j1], ACT.Exp, bias=drift_sb[:, b, t : t + 1]
                 )
 
         def profit_on_vector(b, c, j0=0):
@@ -160,20 +162,20 @@ def tile_list_scenario_profit_store_kernel(
                 ALU.mult,
             )
 
-        def profit_planes(b, c):
-            planes[b, c] = sb([P, PACK, CHUNK], BF16, "planes%d%d" % (b, c))
+        def profit_planes(b, c, over=None):
+            planes[b, c] = sb([P, PACK, CHUNK], BF16, "planes%d%d" % (b, c), over)
             for t in range(PACK):
                 nc.scalar.activation(
                     planes[b, c][:, t, :],
-                    growth[b, c, 0][:, t, :],
+                    plane[b, c, t],
                     ACT.Identity,
                     bias=minus_price[:, b, t : t + 1],
                     scale=price_sb[:, b, t : t + 1],
                 )
 
-        def interleave(b, c):
-            h_rounded[b, c, 0] = sb([P, CHUNK * PACK], BF16, "h_rounded%d%d" % (b, c))[:]
-            nc.scalar.copy(
+        def interleave(b, c, over=None, copy=nc.scalar.copy):
+            h_rounded[b, c, 0] = sb([P, CHUNK * PACK], BF16, "h_rounded%d%d" % (b, c), over)[:]
+            copy(
                 h_rounded[b, c, 0].rearrange("p (g e t) -> p g t e", e=4, t=PACK),
                 planes[b, c][:].rearrange("p t (g e) -> p g t e", e=4),
             )
@@ -240,27 +242,32 @@ def tile_list_scenario_profit_store_kernel(
         quantise_loadings(0, 0, PACK)
         round_loadings(nc.scalar.copy, 1, 0, 0, 0, 2)
         round_loadings(nc.vector.tensor_copy, 1, 0, 0, 2, 4)
-        nc.scalar.activation(minus_price[:], price_sb[:], ACT.Identity, scale=-1.0)
         quantise_loadings(1, 0, 2)
         gather(v_codes(1, 0), tab_w[1][:].bitcast(U32), 0, CHUNK)
-        gather(v_second[0][:, CHUNK:], tab_w[1][:].bitcast(U32), CHUNK, S - CHUNK)
+        gather(v_codes(1, 1), tab_w[1][:].bitcast(U32), CHUNK, 2 * CHUNK)
+        gather(v_codes(1, 2), tab_w[1][:].bitcast(U32), 2 * CHUNK, 3 * CHUNK)
         log_returns(0, 0, (0, 1, 2, 3))
         exponentials(0, 0)
+        nc.scalar.activation(minus_price[:], price_sb[:], ACT.Identity, scale=-1.0)
         log_returns(0, 1, (4, 5))
         exponentials(0, 1)
         profit_planes(0, 1)
         interleave(0, 1)
         log_returns(0, 2, (6, 7))
-        round_loadings(nc.vector.tensor_copy, 0, 1, 0, 0, 2)
-        round_loadings(nc.vector.tensor_copy, 0, 1, 0, 2, 4)
-        quantise_loadings(0, 1, 2, 0, 2)
-        l_rounded[1, 1] = sb([P, PACK * PASS], BF16, "l_rounded11", over="l_raw01_0")
+        exponentials(0, 2, t1=2)
+        round_loadings(nc.vector.tensor_copy, 0, 1, 0)
+        round_loadings(nc.vector.tensor_copy, 0, 1, half, 0, 2)
+        round_loadings(nc.vector.tensor_copy, 0, 1, half, 2, 4)
+        quantise_loadings(0, 1, 2)
+        l_rounded[1, 1] = sb([P, PACK * PASS], BF16, "l_rounded11", over="l_raw01_256")
         round_loadings(nc.vector.tensor_copy, 1, 1, 0)
-        quantise_loadings(0, 1, 2, 2, 4)
         round_loadings(nc.vector.tensor_copy, 1, 1, half)
-        quantise_loadings(1, 1, 1)
+        round_loadings(nc.vector.tensor_copy, 1, 1, last, 0, 2)
+        round_loadings(nc.vector.tensor_copy, 1, 1, last, 2, 4)
+        quantise_loadings(1, 1, 1, 0, 2)
+        quantise_loadings(1, 1, 2, 2, 4)
 
-        h_rounded[0, 0, 0] = l_rounded[1, 1][:, PASS : 3 * PASS]
+        h_rounded[0, 0, 0] = l_rounded[1, 1][:, : 2 * PASS]
         profit_on_vector(0, 0)
         quantise_profit(0, 0)
         log_returns(1, 0, (0, 1, 2, 3))
@@ -276,53 +283,53 @@ def tile_list_scenario_profit_store_kernel(
         quantise_profit(0, 1)
         v_second.append(sb([P, CHUNK], U32, "v_second1", over="h_rounded10_128"))
         gather(v_second[1][:], tab_w[1][:].bitcast(U32), S - CHUNK, S)
-        log_returns(1, 1, (4, 5))
-        exponentials(1, 1)
-        portfolios(0, 0, 2)
-        portfolios(1, 0, 3)
-        portfolios(2, 0, 0)
-        portfolios(3, 0, 0, 1)
+        log_returns(1, 1, (4, 5), order=(2, 0, 3, 1))
+        exponentials(1, 1, over="growth00_0_0")
+        portfolios(0, 0, 0)
+        portfolios(1, 0, 6)
+        portfolios(2, 0, 1)
+        portfolios(3, 0, 1, 1)
+        log_returns(1, 2, (2, 3))
         profit_planes(1, 1)
         place_results(0, 0)
-        exponentials(0, 2, over="growth11_0", t1=2)
         place_results(1, 0)
-        exponentials(0, 2, t0=2)
-        log_returns(1, 2, (2, 3))
-        log_returns(0, 3, (6, 7))
-        interleave(1, 1)
+        exponentials(0, 2, over="h_codes00", t0=2)
+        log_returns(0, 3, (0, 7))
+        interleave(1, 1, over="h_codes10")
         quantise_profit(1, 1)
-        portfolios(0, 1, 1)
-        portfolios(1, 1, 1, 1)
+        portfolios(0, 1, 5)
+        portfolios(1, 1, 5, 1)
         portfolios(2, 1, 4)
         portfolios(3, 1, 4, 1)
         place_results(2, 0, over="planes11")
-        profit_planes(0, 2)
+        profit_planes(0, 2, over="h_scales10")
         place_results(3, 0)
         interleave(0, 2)
         quantise_profit(0, 2)
-        exponentials(1, 2)
+        exponentials(1, 2, over="h_codes00")
         log_returns(1, 3, (2, 3))
         place_results(0, 1)
         profit_planes(1, 2)
         place_results(1, 1)
         interleave(1, 2)
         quantise_profit(1, 2)
-        portfolios(0, 2, 5)
-        portfolios(1, 2, 5, 1)
-        portfolios(2, 2, 0)
+        portfolios(0, 2, 1)
+        portfolios(1, 2, 1, 1)
+        portfolios(2, 2, 6)
         place_results(2, 1, over="planes12")
-        exponentials(0, 3)
+        exponentials(0, 3, over="h_scales10")
         profit_planes(0, 3)
         place_results(3, 1)
         interleave(0, 3)
         quantise_profit(0, 3)
+        exponentials(1, 3, t1=2)
         place_results(0, 2, over="planes03")
-        exponentials(1, 3)
+        exponentials(1, 3, t0=2)
         profit_planes(1, 3)
         place_results(1, 2)
         interleave(1, 3)
         quantise_profit(1, 3)
-        portfolios(0, 3, 1)
+        portfolios(0, 3, 5)
         portfolios(1, 3, 4)
         portfolios(2, 3, 4, 1)
         place_results(2, 2, over="planes13")

@@ -53,7 +53,7 @@ def tile_list_scenario_profit_store_kernel(
         w4_w = sb([P, 2, 2 * N], U8, "w4_w")
         w4_s = sb([P, 2, N], U8, "w4_s")
         wgo_sb = sb([P, S], F32, "wgo_sb")
-        windows = [sb([P, T2], F32, "window%d" % n) for n in range(N // P)]
+        windows = [sb([P, T2], F32, "window%d" % n) for n in range(N // P - 1)]
         banks = [psum.tile([P, BANK], F32, name="bank%d" % i) for i in range(8)]
         l_raw, sums, growth, planes, h_rounded, h_codes, h_scales, y_sums, plane = ({} for i in range(9))
 
@@ -84,9 +84,9 @@ def tile_list_scenario_profit_store_kernel(
         load_loadings(0, 0, 0, PASS)
         load_table_scales(1)
         load_loadings(1, 0, 0, PASS)
+        load_loadings(0, 1, 0, half)
         load_table(1)
         nc.sync.dma_start(drift_sb[:], drift.rearrange("(b p t) -> p b t", b=2, t=PACK))
-        load_loadings(0, 1, 0, half)
         nc.sync.dma_start(price_sb[:], price.rearrange("(b p t) -> p b t", b=2, t=PACK))
         load_loadings(0, 1, half, PASS)
         load_loadings(1, 1, 0, half)
@@ -188,11 +188,12 @@ def tile_list_scenario_profit_store_kernel(
             )
 
         def portfolios(n, c, bank, place=0):
-            y_sums[n, c] = banks[bank][:, CHUNK * place : CHUNK * (place + 1)]
+            y_sums[n, c] = (bank, CHUNK * place, CHUNK)
+            sums_n = banks[bank][:, CHUNK * place : CHUNK * (place + 1)]
             for b in range(2):
                 for j0 in range(0, CHUNK, P):
                     nc.tensor.matmul_mx(
-                        out=y_sums[n, c][:, j0 : j0 + P],
+                        out=sums_n[:, j0 : j0 + P],
                         lhsT=w4_w[:, b, 2 * P * n : 2 * P * (n + 1)].bitcast(FP4X4),
                         lhsT_scale=w4_s[:, b, P * n : P * (n + 1)],
                         rhs=h_codes[b, c][:, j0 : j0 + P].bitcast(FP8X4),
@@ -202,10 +203,10 @@ def tile_list_scenario_profit_store_kernel(
                     )
 
         def portfolios_late(n, bank):
-            y_sums[n, 2] = banks[bank][:]
+            y_sums[n, 2] = (bank, 0, BANK)
             for b in range(2):
                 nc.tensor.matmul_mx(
-                    out=y_sums[n, 2],
+                    out=banks[bank][:],
                     lhsT=w4_w[:, b, 2 * P * n : 2 * P * (n + 1)].bitcast(FP4X4),
                     lhsT_scale=w4_s[:, b, P * n : P * (n + 1)],
                     rhs=late_codes[b][:].bitcast(FP8X4),
@@ -214,13 +215,19 @@ def tile_list_scenario_profit_store_kernel(
                     stop=(b == 1),
                 )
 
-        def place_results(n, c, over=None):
-            width = y_sums[n, c].shape[1]
-            y_sb = sb([P, width], F32, "y_sb%d%d" % (n, c), over)
-            nc.scalar.copy(y_sb[:], y_sums[n, c])
+        def place_results(tiles, c, over=None):
+            bank, place, width = y_sums[tiles[0], c]
+            y_sb = sb([P, width * len(tiles)], F32, "y_sb%d%d" % (tiles[0], c), over)
+            nc.scalar.copy(y_sb[:], banks[bank][:, place : place + width * len(tiles)])
             j0 = CHUNK * c
             entries = scatter_list[:, j0 // GROUP : (j0 + width) // GROUP]
-            nc.vector.tensor_tensor(windows[n][:].indirect(entries), y_sb[:], wgo_sb[:, j0 : j0 + width], ALU.mult)
+            for k, n in enumerate(tiles):
+                nc.vector.tensor_tensor(
+                    windows[n][:].indirect(entries),
+                    y_sb[:, width * k : width * (k + 1)],
+                    wgo_sb[:, j0 : j0 + width],
+                    ALU.mult,
+                )
 
         def store(n):
             nc.sync.dma_start(out[P * n : P * (n + 1), :], windows[n][:])
@@ -232,7 +239,7 @@ def tile_list_scenario_profit_store_kernel(
                 h_scales[b, c] = sb([P, CHUNK], U8, "h_scales%d%d" % (b, c))[:]
                 h_scales[b, c + 2] = late_scales[b][:, CHUNK * c : CHUNK * (c + 1)]
                 h_codes[b, c + 2] = late_codes[b][:, CHUNK * c : CHUNK * (c + 1)]
-        for bc in ((0, 0), (1, 0), (1, 1)):
+        for bc in ((0, 0), (0, 1), (1, 0), (1, 1)):
             h_codes[bc] = sb([P, CHUNK], U32, "h_codes%d%d" % bc)[:]
 
         gather(v_first[:], tab_w[0][:].bitcast(U32), 0, S)
@@ -240,22 +247,22 @@ def tile_list_scenario_profit_store_kernel(
         gather(v_scales[:], tab_s[:], 0, S)
         l_codes[0, 0] = sb([P, PASS], U32, "l_codes00", over="tab_s")
         quantise_loadings(0, 0, PACK)
-        round_loadings(nc.scalar.copy, 1, 0, 0, 0, 2)
-        round_loadings(nc.vector.tensor_copy, 1, 0, 0, 2, 4)
-        quantise_loadings(1, 0, 2)
+        windows.append(sb([P, T2], F32, "window3", over="l_rounded00"))
+        nc.vector.memset(windows[3][:], 0.0)
+        round_loadings(nc.scalar.copy, 1, 0, 0)
         gather(v_codes(1, 0), tab_w[1][:].bitcast(U32), 0, CHUNK)
+        quantise_loadings(1, 0, PACK)
         gather(v_codes(1, 1), tab_w[1][:].bitcast(U32), CHUNK, 2 * CHUNK)
         gather(v_codes(1, 2), tab_w[1][:].bitcast(U32), 2 * CHUNK, 3 * CHUNK)
         log_returns(0, 0, (0, 1, 2, 3))
+        round_loadings(nc.scalar.copy, 0, 1, 0)
         exponentials(0, 0)
         nc.scalar.activation(minus_price[:], price_sb[:], ACT.Identity, scale=-1.0)
         log_returns(0, 1, (4, 5))
         exponentials(0, 1)
         profit_planes(0, 1)
-        interleave(0, 1)
         log_returns(0, 2, (6, 7))
         exponentials(0, 2, t1=2)
-        round_loadings(nc.vector.tensor_copy, 0, 1, 0)
         round_loadings(nc.vector.tensor_copy, 0, 1, half, 0, 2)
         round_loadings(nc.vector.tensor_copy, 0, 1, half, 2, 4)
         quantise_loadings(0, 1, 2)
@@ -279,65 +286,61 @@ def tile_list_scenario_profit_store_kernel(
         profit_on_vector(1, 0, P)
         quantise_profit(1, 0, 0, P)
         quantise_profit(1, 0, P, CHUNK)
-        h_codes[0, 1] = sb([P, CHUNK], U32, "h_codes01", over="h_rounded10_0")[:]
-        quantise_profit(0, 1)
+        interleave(0, 1, over="h_rounded10_0", copy=nc.vector.tensor_copy)
         v_second.append(sb([P, CHUNK], U32, "v_second1", over="h_rounded10_128"))
         gather(v_second[1][:], tab_w[1][:].bitcast(U32), S - CHUNK, S)
+        quantise_profit(0, 1)
         log_returns(1, 1, (4, 5), order=(2, 0, 3, 1))
         exponentials(1, 1, over="growth00_0_0")
         portfolios(0, 0, 0)
         portfolios(1, 0, 6)
-        portfolios(2, 0, 1)
-        portfolios(3, 0, 1, 1)
+        portfolios(2, 0, 4)
+        portfolios(3, 0, 4, 1)
         log_returns(1, 2, (2, 3))
         profit_planes(1, 1)
-        place_results(0, 0)
-        place_results(1, 0)
+        place_results((0,), 0)
+        place_results((1,), 0)
         exponentials(0, 2, over="h_codes00", t0=2)
-        log_returns(0, 3, (0, 7))
+        log_returns(0, 3, (7, 6))
         interleave(1, 1, over="h_codes10")
         quantise_profit(1, 1)
         portfolios(0, 1, 5)
         portfolios(1, 1, 5, 1)
-        portfolios(2, 1, 4)
-        portfolios(3, 1, 4, 1)
-        place_results(2, 0, over="planes11")
+        portfolios(2, 1, 1)
+        portfolios(3, 1, 1, 1)
+        place_results((2, 3), 0, over="planes11")
         profit_planes(0, 2, over="h_scales10")
-        place_results(3, 0)
         interleave(0, 2)
         quantise_profit(0, 2)
-        exponentials(1, 2, over="h_codes00")
+        exponentials(1, 2, over="h_scales00")
         log_returns(1, 3, (2, 3))
-        place_results(0, 1)
+        place_results((0, 1), 1, over="h_scales10")
         profit_planes(1, 2)
-        place_results(1, 1)
         interleave(1, 2)
         quantise_profit(1, 2)
-        portfolios(0, 2, 1)
-        portfolios(1, 2, 1, 1)
-        portfolios(2, 2, 6)
-        place_results(2, 1, over="planes12")
-        exponentials(0, 3, over="h_scales10")
+        portfolios(0, 2, 0)
+        portfolios(1, 2, 0, 1)
+        portfolios(2, 2, 4)
+        place_results((2, 3), 1, over="planes12")
+        exponentials(0, 3, over="h_codes00")
         profit_planes(0, 3)
-        place_results(3, 1)
+        place_results((0,), 2)
         interleave(0, 3)
         quantise_profit(0, 3)
-        exponentials(1, 3, t1=2)
-        place_results(0, 2, over="planes03")
-        exponentials(1, 3, t0=2)
+        exponentials(1, 3, over="h_scales00")
         profit_planes(1, 3)
-        place_results(1, 2)
+        place_results((1,), 2, over="planes03")
         interleave(1, 3)
         quantise_profit(1, 3)
         portfolios(0, 3, 5)
-        portfolios(1, 3, 4)
-        portfolios(2, 3, 4, 1)
-        place_results(2, 2, over="planes13")
-        place_results(0, 3)
+        portfolios(1, 3, 1)
+        portfolios(2, 3, 1, 1)
+        place_results((2,), 2, over="planes13")
+        place_results((0,), 3)
         store(0)
-        for n in (1, 2):
-            place_results(n, 3)
-            store(n)
-        portfolios_late(3, 4)
-        place_results(3, 2)
+        place_results((1, 2), 3)
+        store(1)
+        store(2)
+        portfolios_late(3, 1)
+        place_results((3,), 2)
         store(3)

@@ -249,9 +249,11 @@ def tile_list_scenario_profit_store_kernel(
         quantise_loadings(0, 0, PACK)
         windows.append(sb([P, T2], F32, "window3", over="l_rounded00"))
         nc.vector.memset(windows[3][:], 0.0)
-        round_loadings(nc.scalar.copy, 1, 0, 0)
+        round_loadings(nc.scalar.copy, 1, 0, 0, 0, 2)
+        round_loadings(nc.scalar.copy, 1, 0, 0, 2, 4)
+        quantise_loadings(1, 0, 2, 0, 2)
         gather(v_codes(1, 0), tab_w[1][:].bitcast(U32), 0, CHUNK)
-        quantise_loadings(1, 0, PACK)
+        quantise_loadings(1, 0, 2, 2, 4)
         gather(v_codes(1, 1), tab_w[1][:].bitcast(U32), CHUNK, 2 * CHUNK)
         gather(v_codes(1, 2), tab_w[1][:].bitcast(U32), 2 * CHUNK, 3 * CHUNK)
         log_returns(0, 0, (0, 1, 2, 3))
@@ -260,9 +262,8 @@ def tile_list_scenario_profit_store_kernel(
         nc.scalar.activation(minus_price[:], price_sb[:], ACT.Identity, scale=-1.0)
         log_returns(0, 1, (4, 5))
         exponentials(0, 1)
-        profit_planes(0, 1)
         log_returns(0, 2, (6, 7))
-        exponentials(0, 2, t1=2)
+        exponentials(0, 2)
         round_loadings(nc.vector.tensor_copy, 0, 1, half, 0, 2)
         round_loadings(nc.vector.tensor_copy, 0, 1, half, 2, 4)
         quantise_loadings(0, 1, 2)
@@ -286,13 +287,14 @@ def tile_list_scenario_profit_store_kernel(
         profit_on_vector(1, 0, P)
         quantise_profit(1, 0, 0, P)
         quantise_profit(1, 0, P, CHUNK)
-        interleave(0, 1, over="h_rounded10_0", copy=nc.vector.tensor_copy)
+        h_rounded[0, 1, 0] = sb([P, CHUNK * PACK], BF16, "h_rounded01", over="h_rounded10_0")[:]
+        profit_on_vector(0, 1)
         v_second.append(sb([P, CHUNK], U32, "v_second1", over="h_rounded10_128"))
         gather(v_second[1][:], tab_w[1][:].bitcast(U32), S - CHUNK, S)
         quantise_profit(0, 1)
         log_returns(1, 1, (4, 5), order=(2, 0, 3, 1))
         exponentials(1, 1, over="growth00_0_0")
-        portfolios(0, 0, 0)
+        portfolios(0, 0, 7)
         portfolios(1, 0, 6)
         portfolios(2, 0, 4)
         portfolios(3, 0, 4, 1)
@@ -300,7 +302,6 @@ def tile_list_scenario_profit_store_kernel(
         profit_planes(1, 1)
         place_results((0,), 0)
         place_results((1,), 0)
-        exponentials(0, 2, over="h_codes00", t0=2)
         log_returns(0, 3, (7, 6))
         interleave(1, 1, over="h_codes10")
         quantise_profit(1, 1)
@@ -324,12 +325,12 @@ def tile_list_scenario_profit_store_kernel(
         place_results((2, 3), 1, over="planes12")
         exponentials(0, 3, over="h_codes00")
         profit_planes(0, 3)
-        place_results((0,), 2)
         interleave(0, 3)
         quantise_profit(0, 3)
-        exponentials(1, 3, over="h_scales00")
+        exponentials(1, 3, over="h_scales00", t1=2)
+        place_results((0, 1), 2, over="planes03")
+        exponentials(1, 3, t0=2)
         profit_planes(1, 3)
-        place_results((1,), 2, over="planes03")
         interleave(1, 3)
         quantise_profit(1, 3)
         portfolios(0, 3, 5)

@@ -23,12 +23,16 @@ BANK = 512
 GROUP = 16
 CHUNK = 256
 QUADRANTS = 4
+LINE = 4
+HALF_COLS, LAST_COLS = PASS // 2, PASS - P
+ALL_PLANES, LOW_PLANES, HIGH_PLANES = (0, 4), (0, 2), (2, 4)
 
 
 def tile_list_scenario_profit_store_kernel(
     tc, tab_words, tab_scales, offs, load, drift, price, w4_words, w4_scales, wgo, offs2, out
 ):
     nc = tc.nc
+    on_scalar, on_vector = nc.scalar.copy, nc.vector.tensor_copy
     with ExitStack() as ctx:
         keep = ctx.enter_context(tc.tile_pool(name="keep", bufs=1))
         psum = ctx.enter_context(tc.psum_pool(name="psum", bufs=1))
@@ -40,22 +44,24 @@ def tile_list_scenario_profit_store_kernel(
         scatter_list = sb([P, S // GROUP], U16, "scatter_list")
         tab_w = [sb([P, T], I32, "tab_w%d" % a) for a in range(2)]
         tab_s = sb([P, T], U8, "tab_s")
-        v_first = sb([P, S], U32, "v_first")
-        v_second = [sb([P, S - CHUNK], U32, "v_second0")]
+        v_pass0 = sb([P, S], U32, "v_pass0")
+        v_pass1 = sb([P, S - CHUNK], U32, "v_pass1")
         v_scales = sb([P, S], U8, "v_scales")
-        blocks = [(a, b) for a in range(2) for b in range(2)]
-        l_rounded = {ab: sb([P, PACK * PASS], BF16, "l_rounded%d%d" % ab) for ab in blocks[:3]}
-        l_codes = {ab: sb([P, PASS], U32, "l_codes%d%d" % ab) for ab in blocks[1:]}
-        l_scales = {ab: sb([P, PASS], U8, "l_scales%d%d" % ab) for ab in blocks}
+        v_codes = {(0, c): v_pass0[:, CHUNK * c : CHUNK * (c + 1)] for c in range(4)}
+        for c in range(3):
+            v_codes[1, c] = v_pass1[:, CHUNK * c : CHUNK * (c + 1)]
+        l_rounded = {ab: sb([P, PACK * PASS], BF16, "l_rounded%d%d" % ab) for ab in ((0, 0), (0, 1), (1, 0))}
+        l_codes = {ab: sb([P, PASS], U32, "l_codes%d%d" % ab) for ab in ((0, 1), (1, 0), (1, 1))}
+        l_scales = {(a, b): sb([P, PASS], U8, "l_scales%d%d" % (a, b)) for a in range(2) for b in range(2)}
         drift_sb = sb([P, 2, PACK], F32, "drift_sb")
         price_sb = sb([P, 2, PACK], F32, "price_sb")
         minus_price = sb([P, 2, PACK], F32, "minus_price")
         w4_w = sb([P, 2, 2 * N], U8, "w4_w")
         w4_s = sb([P, 2, N], U8, "w4_s")
         wgo_sb = sb([P, S], F32, "wgo_sb")
-        windows = [sb([P, T2], F32, "window%d" % n) for n in range(N // P - 1)]
+        windows = [sb([P, T2], F32, "window%d" % n) for n in range(3)]
         banks = [psum.tile([P, BANK], F32, name="bank%d" % i) for i in range(8)]
-        l_raw, sums, growth, planes, h_rounded, h_codes, h_scales, y_sums, plane = ({} for i in range(9))
+        l_raw, r_sums, growth, h_planes, h_rounded, h_codes, h_scales, y_place = ({} for i in range(8))
 
         nc.vector.memset(tab_s[:].bitcast(I32), 0)
         nc.vector.memset(w4_s[:].rearrange("p b n -> p (b n)").bitcast(I32), 0)
@@ -77,21 +83,20 @@ def tile_list_scenario_profit_store_kernel(
             rows = load[PASS * a : PASS * (a + 1), PASS * b + col0 : PASS * b + col1]
             nc.sync.dma_start(l_raw[a, b, col0][:], rows.rearrange("(p i) c -> p i c", i=PACK))
 
-        half, last = PASS // 2, PASS - P
         load_table(0)
         nc.sync.dma_start(gather_list[:], offs)
         load_table_scales(0)
         load_loadings(0, 0, 0, PASS)
         load_table_scales(1)
         load_loadings(1, 0, 0, PASS)
-        load_loadings(0, 1, 0, half)
+        load_loadings(0, 1, 0, HALF_COLS)
         load_table(1)
         nc.sync.dma_start(drift_sb[:], drift.rearrange("(b p t) -> p b t", b=2, t=PACK))
         nc.sync.dma_start(price_sb[:], price.rearrange("(b p t) -> p b t", b=2, t=PACK))
-        load_loadings(0, 1, half, PASS)
-        load_loadings(1, 1, 0, half)
-        load_loadings(1, 1, half, last)
-        load_loadings(1, 1, last, PASS)
+        load_loadings(0, 1, HALF_COLS, PASS)
+        load_loadings(1, 1, 0, HALF_COLS)
+        load_loadings(1, 1, HALF_COLS, LAST_COLS)
+        load_loadings(1, 1, LAST_COLS, PASS)
         nc.sync.dma_start(wgo_sb[:], wgo)
         nc.sync.dma_start(scatter_list[:], offs2)
         nc.sync.dma_start(w4_w[:].bitcast(I32), w4_words.rearrange("b p c -> p b c").bitcast(I32))
@@ -102,82 +107,73 @@ def tile_list_scenario_profit_store_kernel(
             )
 
         def gather(dst, window, j0, j1):
-            entries = gather_list[:, j0 // GROUP : j1 // GROUP]
-            nc.vector.tensor_copy(dst, window.indirect(entries))
+            nc.vector.tensor_copy(dst, window.indirect(gather_list[:, j0 // GROUP : j1 // GROUP]))
 
-        def round_loadings(copy, a, b, col0, t0=0, t1=PACK):
-            piece = l_raw[a, b, col0]
+        def gather_second_pass(c):
+            gather(v_codes[1, c], tab_w[1][:].bitcast(U32), CHUNK * c, CHUNK * (c + 1))
+
+        def round_loadings(copy, a, b, col0, planes=ALL_PLANES):
+            piece, (t0, t1) = l_raw[a, b, col0], planes
             m0, m1 = col0 // PACK, (col0 + piece.shape[2]) // PACK
             copy(
                 l_rounded[a, b][:].rearrange("p (t m i) -> p m i t", t=PACK, i=PACK)[:, m0:m1, :, t0:t1],
                 piece[:].rearrange("p i (m t) -> p m i t", t=PACK)[:, :, :, t0:t1],
             )
 
-        def quantise_loadings(a, b, planes, t0=0, t1=PACK):
-            for t in range(t0, t1, planes):
-                nc.vector.quantize_mx(
-                    out=l_codes[a, b][:, P * t : P * (t + planes)].bitcast(FP8X4),
-                    scales=l_scales[a, b][:, P * t : P * (t + planes)],
-                    in_=l_rounded[a, b][:, PASS * t : PASS * (t + planes)],
-                )
+        def quantise_loadings(a, b, planes):
+            t0, t1 = planes
+            nc.vector.quantize_mx(
+                out=l_codes[a, b][:, P * t0 : P * t1].bitcast(FP8X4),
+                scales=l_scales[a, b][:, P * t0 : P * t1],
+                in_=l_rounded[a, b][:, PASS * t0 : PASS * t1],
+            )
 
-        def v_codes(a, c):
-            if a == 0:
-                return v_first[:, CHUNK * c : CHUNK * (c + 1)]
-            return v_second[c // 3][:, CHUNK * (c % 3) : CHUNK * (c % 3 + 1)]
-
-        def log_returns(b, c, used, order=range(PACK)):
-            cols = slice(CHUNK * c, CHUNK * (c + 1))
+        def log_returns(b, c, used, order=(0, 1, 2, 3)):
             share = PACK // len(used)
             for k, t in enumerate(order):
                 place = CHUNK * (k % share)
-                sums[b, c, t] = banks[used[k // share]][:, place : place + CHUNK]
+                r_sums[b, c, t] = banks[used[k // share]][:, place : place + CHUNK]
                 for a in range(2):
                     nc.tensor.matmul_mx(
-                        out=sums[b, c, t],
+                        out=r_sums[b, c, t],
                         lhsT=l_codes[a, b][:, P * t : P * (t + 1)].bitcast(FP8X4),
                         lhsT_scale=l_scales[a, b][:, P * t : P * (t + 1)],
-                        rhs=v_codes(a, c).bitcast(FP8X4),
-                        rhs_scale=v_scales[4 * a : P, cols],
+                        rhs=v_codes[a, c].bitcast(FP8X4),
+                        rhs_scale=v_scales[4 * a : P, CHUNK * c : CHUNK * (c + 1)],
                         start=(a == 0),
                         stop=(a == 1),
                     )
 
-        def exponentials(b, c, j0=0, j1=CHUNK, over=None, t0=0, t1=PACK):
-            growth[b, c, j0] = sb([P, t1 - t0, j1 - j0], F32, "growth%d%d_%d_%d" % (b, c, j0, t0), over)
+        def exponentials(b, c, planes=ALL_PLANES, over=None):
+            t0, t1 = planes
+            dst = sb([P, t1 - t0, CHUNK], F32, "growth%d%d_%d" % (b, c, t0), over)
             for t in range(t0, t1):
-                plane[b, c, t] = growth[b, c, j0][:, t - t0, :]
-                nc.scalar.activation(
-                    plane[b, c, t], sums[b, c, t][:, j0:j1], ACT.Exp, bias=drift_sb[:, b, t : t + 1]
-                )
+                growth[b, c, t] = dst[:, t - t0, :]
+                nc.scalar.activation(growth[b, c, t], r_sums[b, c, t], ACT.Exp, bias=drift_sb[:, b, t : t + 1])
 
-        def profit_on_vector(b, c, j0=0):
-            width = growth[b, c, j0].shape[2]
-            nc.vector.scalar_tensor_tensor(
-                h_rounded[b, c, j0].rearrange("p (j t) -> p j t", t=PACK),
-                growth[b, c, j0][:].rearrange("p t j -> p j t"),
-                -1.0,
-                price_sb[:, b, :].unsqueeze(1).to_broadcast([P, width, PACK]),
-                ALU.add,
-                ALU.mult,
-            )
-
-        def profit_planes(b, c, over=None):
-            planes[b, c] = sb([P, PACK, CHUNK], BF16, "planes%d%d" % (b, c), over)
+        def profit_on_scalar(b, c, over=None):
+            h_planes[b, c] = sb([P, PACK, CHUNK], BF16, "h_planes%d%d" % (b, c), over)
             for t in range(PACK):
                 nc.scalar.activation(
-                    planes[b, c][:, t, :],
-                    plane[b, c, t],
+                    h_planes[b, c][:, t, :],
+                    growth[b, c, t],
                     ACT.Identity,
                     bias=minus_price[:, b, t : t + 1],
                     scale=price_sb[:, b, t : t + 1],
                 )
 
-        def interleave(b, c, over=None, copy=nc.scalar.copy):
-            h_rounded[b, c, 0] = sb([P, CHUNK * PACK], BF16, "h_rounded%d%d" % (b, c), over)[:]
+        def profit_on_vector(b, c, dst):
+            h_planes[b, c] = dst
+            for t in range(PACK):
+                nc.vector.tensor_scalar(
+                    dst[:, t, :], growth[b, c, t], -1.0, price_sb[:, b, t : t + 1], ALU.add, ALU.mult
+                )
+
+        def interleave(copy, b, c, j0=0, j1=CHUNK, over=None):
+            h_rounded[b, c, j0] = sb([P, (j1 - j0) * PACK], BF16, "h_rounded%d%d_%d" % (b, c, j0), over)[:]
             copy(
-                h_rounded[b, c, 0].rearrange("p (g e t) -> p g t e", e=4, t=PACK),
-                planes[b, c][:].rearrange("p t (g e) -> p g t e", e=4),
+                h_rounded[b, c, j0].rearrange("p (g e t) -> p g t e", e=LINE, t=PACK),
+                h_planes[b, c][:, :, j0:j1].rearrange("p t (g e) -> p g t e", e=LINE),
             )
 
         def quantise_profit(b, c, j0=0, j1=CHUNK):
@@ -187,44 +183,42 @@ def tile_list_scenario_profit_store_kernel(
                 in_=h_rounded[b, c, j0],
             )
 
-        def portfolios(n, c, bank, place=0):
-            y_sums[n, c] = (bank, CHUNK * place, CHUNK)
-            sums_n = banks[bank][:, CHUNK * place : CHUNK * (place + 1)]
-            for b in range(2):
-                for j0 in range(0, CHUNK, P):
-                    nc.tensor.matmul_mx(
-                        out=sums_n[:, j0 : j0 + P],
-                        lhsT=w4_w[:, b, 2 * P * n : 2 * P * (n + 1)].bitcast(FP4X4),
-                        lhsT_scale=w4_s[:, b, P * n : P * (n + 1)],
-                        rhs=h_codes[b, c][:, j0 : j0 + P].bitcast(FP8X4),
-                        rhs_scale=h_scales[b, c][:, j0 : j0 + P],
-                        start=(b == 0 and j0 == 0),
-                        stop=(b == 1 and j0 == CHUNK - P),
-                    )
+        def second_product(dst, n, b, codes, scales, start, stop):
+            nc.tensor.matmul_mx(
+                out=dst,
+                lhsT=w4_w[:, b, 2 * P * n : 2 * P * (n + 1)].bitcast(FP4X4),
+                lhsT_scale=w4_s[:, b, P * n : P * (n + 1)],
+                rhs=codes.bitcast(FP8X4),
+                rhs_scale=scales,
+                start=start,
+                stop=stop,
+            )
 
-        def portfolios_late(n, bank):
-            y_sums[n, 2] = (bank, 0, BANK)
-            for b in range(2):
-                nc.tensor.matmul_mx(
-                    out=banks[bank][:],
-                    lhsT=w4_w[:, b, 2 * P * n : 2 * P * (n + 1)].bitcast(FP4X4),
-                    lhsT_scale=w4_s[:, b, P * n : P * (n + 1)],
-                    rhs=late_codes[b][:].bitcast(FP8X4),
-                    rhs_scale=late_scales[b][:],
-                    start=(b == 0),
-                    stop=(b == 1),
-                )
+        def portfolios(tiles, c, bank):
+            y_place[tiles, c] = banks[bank][:, : CHUNK * len(tiles)]
+            for place, n in enumerate(tiles):
+                for b in range(2):
+                    for j0 in (0, P):
+                        second_product(
+                            banks[bank][:, CHUNK * place + j0 : CHUNK * place + j0 + P],
+                            n,
+                            b,
+                            h_codes[b, c][:, j0 : j0 + P],
+                            h_scales[b, c][:, j0 : j0 + P],
+                            start=(b == 0 and j0 == 0),
+                            stop=(b == 1 and j0 == P),
+                        )
 
         def place_results(tiles, c, over=None):
-            bank, place, width = y_sums[tiles[0], c]
-            y_sb = sb([P, width * len(tiles)], F32, "y_sb%d%d" % (tiles[0], c), over)
-            nc.scalar.copy(y_sb[:], banks[bank][:, place : place + width * len(tiles)])
-            j0 = CHUNK * c
+            y_sums = y_place[tiles, c]
+            width, j0 = y_sums.shape[1] // len(tiles), CHUNK * c
+            y_sb = sb([P, y_sums.shape[1]], F32, "y_sb%d%d" % (tiles[0], c), over)
+            nc.scalar.copy(y_sb[:], y_sums)
             entries = scatter_list[:, j0 // GROUP : (j0 + width) // GROUP]
-            for k, n in enumerate(tiles):
+            for place, n in enumerate(tiles):
                 nc.vector.tensor_tensor(
                     windows[n][:].indirect(entries),
-                    y_sb[:, width * k : width * (k + 1)],
+                    y_sb[:, width * place : width * (place + 1)],
                     wgo_sb[:, j0 : j0 + width],
                     ALU.mult,
                 )
@@ -239,109 +233,112 @@ def tile_list_scenario_profit_store_kernel(
                 h_scales[b, c] = sb([P, CHUNK], U8, "h_scales%d%d" % (b, c))[:]
                 h_scales[b, c + 2] = late_scales[b][:, CHUNK * c : CHUNK * (c + 1)]
                 h_codes[b, c + 2] = late_codes[b][:, CHUNK * c : CHUNK * (c + 1)]
-        for bc in ((0, 0), (0, 1), (1, 0), (1, 1)):
-            h_codes[bc] = sb([P, CHUNK], U32, "h_codes%d%d" % bc)[:]
+        for b in range(2):
+            for c in range(2):
+                h_codes[b, c] = sb([P, CHUNK], U32, "h_codes%d%d" % (b, c))[:]
 
-        gather(v_first[:], tab_w[0][:].bitcast(U32), 0, S)
-        round_loadings(nc.scalar.copy, 0, 0, 0)
+        gather(v_pass0[:], tab_w[0][:].bitcast(U32), 0, S)
+        round_loadings(on_scalar, 0, 0, 0)
         gather(v_scales[:], tab_s[:], 0, S)
         l_codes[0, 0] = sb([P, PASS], U32, "l_codes00", over="tab_s")
-        quantise_loadings(0, 0, PACK)
+        quantise_loadings(0, 0, ALL_PLANES)
         windows.append(sb([P, T2], F32, "window3", over="l_rounded00"))
         nc.vector.memset(windows[3][:], 0.0)
-        round_loadings(nc.scalar.copy, 1, 0, 0, 0, 2)
-        round_loadings(nc.scalar.copy, 1, 0, 0, 2, 4)
-        quantise_loadings(1, 0, 2, 0, 2)
-        gather(v_codes(1, 0), tab_w[1][:].bitcast(U32), 0, CHUNK)
-        quantise_loadings(1, 0, 2, 2, 4)
-        gather(v_codes(1, 1), tab_w[1][:].bitcast(U32), CHUNK, 2 * CHUNK)
-        gather(v_codes(1, 2), tab_w[1][:].bitcast(U32), 2 * CHUNK, 3 * CHUNK)
+        round_loadings(on_scalar, 1, 0, 0, LOW_PLANES)
+        round_loadings(on_scalar, 1, 0, 0, HIGH_PLANES)
+        quantise_loadings(1, 0, LOW_PLANES)
+        gather_second_pass(0)
+        quantise_loadings(1, 0, HIGH_PLANES)
+        gather_second_pass(1)
+        gather_second_pass(2)
         log_returns(0, 0, (0, 1, 2, 3))
-        round_loadings(nc.scalar.copy, 0, 1, 0)
+        round_loadings(on_scalar, 0, 1, 0)
         exponentials(0, 0)
         nc.scalar.activation(minus_price[:], price_sb[:], ACT.Identity, scale=-1.0)
         log_returns(0, 1, (4, 5))
         exponentials(0, 1)
+        profit_on_scalar(0, 1)
         log_returns(0, 2, (6, 7))
-        exponentials(0, 2)
-        round_loadings(nc.vector.tensor_copy, 0, 1, half, 0, 2)
-        round_loadings(nc.vector.tensor_copy, 0, 1, half, 2, 4)
-        quantise_loadings(0, 1, 2)
-        l_rounded[1, 1] = sb([P, PACK * PASS], BF16, "l_rounded11", over="l_raw01_256")
-        round_loadings(nc.vector.tensor_copy, 1, 1, 0)
-        round_loadings(nc.vector.tensor_copy, 1, 1, half)
-        round_loadings(nc.vector.tensor_copy, 1, 1, last, 0, 2)
-        round_loadings(nc.vector.tensor_copy, 1, 1, last, 2, 4)
-        quantise_loadings(1, 1, 1, 0, 2)
-        quantise_loadings(1, 1, 2, 2, 4)
+        exponentials(0, 2, LOW_PLANES)
 
-        h_rounded[0, 0, 0] = l_rounded[1, 1][:, : 2 * PASS]
-        profit_on_vector(0, 0)
-        quantise_profit(0, 0)
+        round_loadings(on_vector, 0, 1, HALF_COLS, LOW_PLANES)
+        round_loadings(on_vector, 0, 1, HALF_COLS, HIGH_PLANES)
+        quantise_loadings(0, 1, LOW_PLANES)
+        quantise_loadings(0, 1, HIGH_PLANES)
+        l_rounded[1, 1] = sb([P, PACK * PASS], BF16, "l_rounded11", over="l_raw01_%d" % HALF_COLS)
+        round_loadings(on_vector, 1, 1, 0)
+        round_loadings(on_vector, 1, 1, HALF_COLS)
+        round_loadings(on_vector, 1, 1, LAST_COLS, LOW_PLANES)
+        round_loadings(on_vector, 1, 1, LAST_COLS, HIGH_PLANES)
+        for planes in ((0, 1), (1, 2), HIGH_PLANES):
+            quantise_loadings(1, 1, planes)
+
+        profit_on_vector(0, 0, l_rounded[1, 1][:, : 2 * PASS].rearrange("p (t j) -> p t j", t=PACK))
+        interleave(on_vector, 0, 0)
         log_returns(1, 0, (0, 1, 2, 3))
-        exponentials(1, 0, 0, P)
-        exponentials(1, 0, P, CHUNK)
+        exponentials(1, 0)
+        profit_on_vector(1, 0, sb([P, PACK, CHUNK], BF16, "h_planes10"))
+        quantise_profit(0, 0)
         for j0 in (0, P):
-            h_rounded[1, 0, j0] = sb([P, P * PACK], BF16, "h_rounded10_%d" % j0)[:]
-        profit_on_vector(1, 0, 0)
-        profit_on_vector(1, 0, P)
-        quantise_profit(1, 0, 0, P)
-        quantise_profit(1, 0, P, CHUNK)
-        h_rounded[0, 1, 0] = sb([P, CHUNK * PACK], BF16, "h_rounded01", over="h_rounded10_0")[:]
-        profit_on_vector(0, 1)
-        v_second.append(sb([P, CHUNK], U32, "v_second1", over="h_rounded10_128"))
-        gather(v_second[1][:], tab_w[1][:].bitcast(U32), S - CHUNK, S)
+            interleave(on_vector, 1, 0, j0, j0 + P)
+        for j0 in (0, P):
+            quantise_profit(1, 0, j0, j0 + P)
+        interleave(on_vector, 0, 1, over="h_rounded10_0")
+        v_codes[1, 3] = sb([P, CHUNK], U32, "v_pass1_last", over="h_rounded10_%d" % P)[:]
+        gather_second_pass(3)
         quantise_profit(0, 1)
         log_returns(1, 1, (4, 5), order=(2, 0, 3, 1))
-        exponentials(1, 1, over="growth00_0_0")
-        portfolios(0, 0, 7)
-        portfolios(1, 0, 6)
-        portfolios(2, 0, 4)
-        portfolios(3, 0, 4, 1)
+        exponentials(1, 1, over="growth00_0")
+        portfolios((0,), 0, 0)
+        portfolios((1,), 0, 6)
+        portfolios((2, 3), 0, 4)
         log_returns(1, 2, (2, 3))
-        profit_planes(1, 1)
+        profit_on_scalar(1, 1)
         place_results((0,), 0)
         place_results((1,), 0)
+
+        exponentials(0, 2, HIGH_PLANES, over="h_codes00")
         log_returns(0, 3, (7, 6))
-        interleave(1, 1, over="h_codes10")
+        interleave(on_scalar, 1, 1, over="h_codes10")
         quantise_profit(1, 1)
-        portfolios(0, 1, 5)
-        portfolios(1, 1, 5, 1)
-        portfolios(2, 1, 1)
-        portfolios(3, 1, 1, 1)
-        place_results((2, 3), 0, over="planes11")
-        profit_planes(0, 2, over="h_scales10")
-        interleave(0, 2)
+        portfolios((0, 1), 1, 5)
+        portfolios((2, 3), 1, 1)
+        place_results((2, 3), 0, over="h_planes11")
+
+        profit_on_scalar(0, 2, over="h_scales10")
+        interleave(on_scalar, 0, 2)
         quantise_profit(0, 2)
         exponentials(1, 2, over="h_scales00")
         log_returns(1, 3, (2, 3))
         place_results((0, 1), 1, over="h_scales10")
-        profit_planes(1, 2)
-        interleave(1, 2)
+        profit_on_scalar(1, 2)
+        interleave(on_scalar, 1, 2)
         quantise_profit(1, 2)
-        portfolios(0, 2, 0)
-        portfolios(1, 2, 0, 1)
-        portfolios(2, 2, 4)
-        place_results((2, 3), 1, over="planes12")
+        portfolios((0, 1), 2, 0)
+        portfolios((2,), 2, 4)
+        place_results((2, 3), 1, over="h_planes12")
+
         exponentials(0, 3, over="h_codes00")
-        profit_planes(0, 3)
-        interleave(0, 3)
+        profit_on_scalar(0, 3)
+        interleave(on_scalar, 0, 3)
         quantise_profit(0, 3)
-        exponentials(1, 3, over="h_scales00", t1=2)
-        place_results((0, 1), 2, over="planes03")
-        exponentials(1, 3, t0=2)
-        profit_planes(1, 3)
-        interleave(1, 3)
+        exponentials(1, 3, LOW_PLANES, over="h_scales00")
+        place_results((0, 1), 2, over="h_planes03")
+        exponentials(1, 3, HIGH_PLANES)
+        profit_on_scalar(1, 3)
+        interleave(on_scalar, 1, 3)
         quantise_profit(1, 3)
-        portfolios(0, 3, 5)
-        portfolios(1, 3, 1)
-        portfolios(2, 3, 1, 1)
-        place_results((2,), 2, over="planes13")
+        portfolios((0,), 3, 5)
+        portfolios((1, 2), 3, 1)
+
+        place_results((2,), 2, over="h_planes13")
         place_results((0,), 3)
         store(0)
         place_results((1, 2), 3)
         store(1)
         store(2)
-        portfolios_late(3, 1)
+        for b in range(2):
+            second_product(banks[1][:], 3, b, late_codes[b][:], late_scales[b][:], start=(b == 0), stop=(b == 1))
+        y_place[(3,), 2] = banks[1][:]
         place_results((3,), 2)
         store(3)

@@ -59,7 +59,7 @@ def tile_list_scenario_profit_store_kernel(
         w4_w = sb([P, 2, 2 * N], U8, "w4_w")
         w4_s = sb([P, 2, N], U8, "w4_s")
         wgo_sb = sb([P, S], F32, "wgo_sb")
-        windows = [sb([P, T2], F32, "window%d" % n) for n in range(3)]
+        windows = [sb([P, T2], F32, "window%d" % n) for n in range(2)]
         banks = [psum.tile([P, BANK], F32, name="bank%d" % i) for i in range(8)]
         l_raw, r_sums, growth, h_planes, h_rounded, h_codes, h_scales, y_place = ({} for i in range(8))
 
@@ -238,12 +238,12 @@ def tile_list_scenario_profit_store_kernel(
                 h_codes[b, c] = sb([P, CHUNK], U32, "h_codes%d%d" % (b, c))[:]
 
         gather(v_pass0[:], tab_w[0][:].bitcast(U32), 0, S)
+        last_window = sb([P, T2], F32, "window3", over="tab_w0")
+        nc.gpsimd.memset(last_window[:], 0.0)
         round_loadings(on_scalar, 0, 0, 0)
         gather(v_scales[:], tab_s[:], 0, S)
         l_codes[0, 0] = sb([P, PASS], U32, "l_codes00", over="tab_s")
         quantise_loadings(0, 0, ALL_PLANES)
-        windows.append(sb([P, T2], F32, "window3", over="l_rounded00"))
-        nc.vector.memset(windows[3][:], 0.0)
         round_loadings(on_scalar, 1, 0, 0, LOW_PLANES)
         round_loadings(on_scalar, 1, 0, 0, HIGH_PLANES)
         quantise_loadings(1, 0, LOW_PLANES)
@@ -287,6 +287,8 @@ def tile_list_scenario_profit_store_kernel(
         v_codes[1, 3] = sb([P, CHUNK], U32, "v_pass1_last", over="h_rounded10_%d" % P)[:]
         gather_second_pass(3)
         quantise_profit(0, 1)
+        windows.extend([sb([P, T2], F32, "window2", over="h_rounded10_0"), last_window])
+        nc.gpsimd.memset(windows[2][:], 0.0)
         log_returns(1, 1, (4, 5), order=(2, 0, 3, 1))
         exponentials(1, 1, over="growth00_0")
         portfolios((0,), 0, 0)

@@ -22,7 +22,6 @@ PASS = P * PACK
 BANK = 512
 GROUP = 16
 CHUNK = 256
-QUADRANTS = 4
 LINE = 4
 HALF_COLS, LAST_COLS = PASS // 2, PASS - P
 ALL_PLANES, LOW_PLANES, HIGH_PLANES = (0, 4), (0, 2), (2, 4)
@@ -71,12 +70,12 @@ def tile_list_scenario_profit_store_kernel(
         def load_table(a):
             nc.sync.dma_start(tab_w[a][:], tab_words[a].rearrange("p t i -> p (t i)").bitcast(I32))
 
-        def load_table_scales(a):
-            for q in range(QUADRANTS):
-                row = 32 * q + 4 * a
-                nc.sync.dma_start(
-                    tab_s[row : row + 4, :].bitcast(I32), tab_scales[a, 4 * q : 4 * q + 4, :].bitcast(I32)
-                )
+        def load_table_scales(rows):
+            for r in rows:
+                for a in range(2):
+                    nc.sync.dma_start(
+                        tab_s[4 * a + r : P : 32, :].bitcast(I32), tab_scales[a, r : 16 : 4, :].bitcast(I32)
+                    )
 
         def load_loadings(a, b, col0, col1):
             l_raw[a, b, col0] = sb([P, PACK, col1 - col0], F32, "l_raw%d%d_%d" % (a, b, col0))
@@ -85,9 +84,9 @@ def tile_list_scenario_profit_store_kernel(
 
         load_table(0)
         nc.sync.dma_start(gather_list[:], offs)
-        load_table_scales(0)
+        load_table_scales((0, 1))
         load_loadings(0, 0, 0, PASS)
-        load_table_scales(1)
+        load_table_scales((2, 3))
         load_loadings(1, 0, 0, PASS)
         load_loadings(0, 1, 0, HALF_COLS)
         load_table(1)
@@ -100,10 +99,10 @@ def tile_list_scenario_profit_store_kernel(
         nc.sync.dma_start(wgo_sb[:], wgo)
         nc.sync.dma_start(scatter_list[:], offs2)
         nc.sync.dma_start(w4_w[:].bitcast(I32), w4_words.rearrange("b p c -> p b c").bitcast(I32))
-        for q in range(QUADRANTS):
+        for r in range(4):
             nc.sync.dma_start(
-                w4_s[32 * q : 32 * q + 4, :, :].bitcast(I32),
-                w4_scales[:, 4 * q : 4 * q + 4, :].rearrange("b r n -> r b n").bitcast(I32),
+                w4_s[r:P:32, :, :].bitcast(I32),
+                w4_scales[:, r:16:4, :].rearrange("b q n -> q b n").bitcast(I32),
             )
 
         def gather(dst, window, j0, j1):

@@ -223,7 +223,8 @@ def tile_list_scenario_profit_store_kernel(
                 )
 
         def store(n):
-            nc.sync.dma_start(out[P * n : P * (n + 1), :], windows[n][:])
+            queue = nc.scalar if n % 2 else nc.sync
+            queue.dma_start(out[P * n : P * (n + 1), :], windows[n][:])
 
         late_codes = [sb([P, 2 * CHUNK], U32, "late_codes%d" % b) for b in range(2)]
         late_scales = [sb([P, 2 * CHUNK], U8, "late_scales%d" % b) for b in range(2)]

@@ -88,8 +88,8 @@ def tile_list_scenario_profit_store_kernel(
         load_loadings(0, 0, 0, PASS)
         load_table_scales((2, 3))
         load_loadings(1, 0, 0, PASS)
-        load_loadings(0, 1, 0, HALF_COLS)
         load_table(1)
+        load_loadings(0, 1, 0, HALF_COLS)
         nc.sync.dma_start(drift_sb[:], drift.rearrange("(b p t) -> p b t", b=2, t=PACK))
         nc.sync.dma_start(price_sb[:], price.rearrange("(b p t) -> p b t", b=2, t=PACK))
         load_loadings(0, 1, HALF_COLS, PASS)

@@ -44,10 +44,10 @@ def tile_list_scenario_profit_store_kernel(
         tab_w = [sb([P, T], I32, "tab_w%d" % a) for a in range(2)]
         tab_s = sb([P, T], U8, "tab_s")
         v_pass0 = sb([P, S], U32, "v_pass0")
-        v_pass1 = sb([P, S - CHUNK], U32, "v_pass1")
+        v_pass1 = sb([P, S], U32, "v_pass1")
         v_scales = sb([P, S], U8, "v_scales")
         v_codes = {(0, c): v_pass0[:, CHUNK * c : CHUNK * (c + 1)] for c in range(4)}
-        for c in range(3):
+        for c in range(4):
             v_codes[1, c] = v_pass1[:, CHUNK * c : CHUNK * (c + 1)]
         l_rounded = {ab: sb([P, PACK * PASS], BF16, "l_rounded%d%d" % ab) for ab in ((0, 0), (0, 1), (1, 0))}
         l_codes = {ab: sb([P, PASS], U32, "l_codes%d%d" % ab) for ab in ((0, 1), (1, 0), (1, 1))}
@@ -91,8 +91,8 @@ def tile_list_scenario_profit_store_kernel(
         load_table(1)
         load_loadings(0, 1, 0, HALF_COLS)
         nc.sync.dma_start(drift_sb[:], drift.rearrange("(b p t) -> p b t", b=2, t=PACK))
-        nc.sync.dma_start(price_sb[:], price.rearrange("(b p t) -> p b t", b=2, t=PACK))
         load_loadings(0, 1, HALF_COLS, PASS)
+        nc.sync.dma_start(price_sb[:], price.rearrange("(b p t) -> p b t", b=2, t=PACK))
         load_loadings(1, 1, 0, HALF_COLS)
         load_loadings(1, 1, HALF_COLS, LAST_COLS)
         load_loadings(1, 1, LAST_COLS, PASS)
@@ -111,12 +111,14 @@ def tile_list_scenario_profit_store_kernel(
         def gather_second_pass(c):
             gather(v_codes[1, c], tab_w[1][:].bitcast(U32), CHUNK * c, CHUNK * (c + 1))
 
-        def round_loadings(copy, a, b, col0, planes=ALL_PLANES):
-            piece, (t0, t1) = l_raw[a, b, col0], planes
+        def round_loadings(copy, a, b, col0, planes=ALL_PLANES, part=None):
+            piece, (t0, t1) = l_raw[a, b, col0][:], planes
+            if part is not None:
+                piece, col0 = piece[:, :, part[0] : part[1]], col0 + part[0]
             m0, m1 = col0 // PACK, (col0 + piece.shape[2]) // PACK
             copy(
                 l_rounded[a, b][:].rearrange("p (t m i) -> p m i t", t=PACK, i=PACK)[:, m0:m1, :, t0:t1],
-                piece[:].rearrange("p i (m t) -> p m i t", t=PACK)[:, :, :, t0:t1],
+                piece.rearrange("p i (m t) -> p m i t", t=PACK)[:, :, :, t0:t1],
             )
 
         def quantise_loadings(a, b, planes):
@@ -245,12 +247,12 @@ def tile_list_scenario_profit_store_kernel(
         l_codes[0, 0] = sb([P, PASS], U32, "l_codes00", over="tab_s")
         quantise_loadings(0, 0, ALL_PLANES)
         round_loadings(on_scalar, 1, 0, 0, LOW_PLANES)
-        round_loadings(on_scalar, 1, 0, 0, HIGH_PLANES)
+        round_loadings(on_scalar, 1, 0, 0, HIGH_PLANES, (0, HALF_COLS))
+        round_loadings(on_vector, 1, 0, 0, HIGH_PLANES, (HALF_COLS, PASS))
         quantise_loadings(1, 0, LOW_PLANES)
         gather_second_pass(0)
         quantise_loadings(1, 0, HIGH_PLANES)
-        gather_second_pass(1)
-        gather_second_pass(2)
+        gather(v_pass1[:, CHUNK:], tab_w[1][:].bitcast(U32), CHUNK, S)
         log_returns(0, 0, (0, 1, 2, 3))
         round_loadings(on_scalar, 0, 1, 0)
         exponentials(0, 0)
@@ -284,8 +286,6 @@ def tile_list_scenario_profit_store_kernel(
         for j0 in (0, P):
             quantise_profit(1, 0, j0, j0 + P)
         interleave(on_vector, 0, 1, over="h_rounded10_0")
-        v_codes[1, 3] = sb([P, CHUNK], U32, "v_pass1_last", over="h_rounded10_%d" % P)[:]
-        gather_second_pass(3)
         quantise_profit(0, 1)
         windows.extend([sb([P, T2], F32, "window2", over="h_rounded10_0"), last_window])
         nc.gpsimd.memset(windows[2][:], 0.0)

@@ -43,12 +43,8 @@ def tile_list_scenario_profit_store_kernel(
         scatter_list = sb([P, S // GROUP], U16, "scatter_list")
         tab_w = [sb([P, T], I32, "tab_w%d" % a) for a in range(2)]
         tab_s = sb([P, T], U8, "tab_s")
-        v_pass0 = sb([P, S], U32, "v_pass0")
-        v_pass1 = sb([P, S], U32, "v_pass1")
+        v_words = [sb([P, S], U32, "v_words%d" % a) for a in range(2)]
         v_scales = sb([P, S], U8, "v_scales")
-        v_codes = {(0, c): v_pass0[:, CHUNK * c : CHUNK * (c + 1)] for c in range(4)}
-        for c in range(4):
-            v_codes[1, c] = v_pass1[:, CHUNK * c : CHUNK * (c + 1)]
         l_rounded = {ab: sb([P, PACK * PASS], BF16, "l_rounded%d%d" % ab) for ab in ((0, 0), (0, 1), (1, 0))}
         l_codes = {ab: sb([P, PASS], U32, "l_codes%d%d" % ab) for ab in ((0, 1), (1, 0), (1, 1))}
         l_scales = {(a, b): sb([P, PASS], U8, "l_scales%d%d" % (a, b)) for a in range(2) for b in range(2)}
@@ -108,17 +104,16 @@ def tile_list_scenario_profit_store_kernel(
         def gather(dst, window, j0, j1):
             nc.vector.tensor_copy(dst, window.indirect(gather_list[:, j0 // GROUP : j1 // GROUP]))
 
-        def gather_second_pass(c):
-            gather(v_codes[1, c], tab_w[1][:].bitcast(U32), CHUNK * c, CHUNK * (c + 1))
+        def gather_words(a, j0, j1):
+            gather(v_words[a][:, j0:j1], tab_w[a][:].bitcast(U32), j0, j1)
 
-        def round_loadings(copy, a, b, col0, planes=ALL_PLANES, part=None):
-            piece, (t0, t1) = l_raw[a, b, col0][:], planes
-            if part is not None:
-                piece, col0 = piece[:, :, part[0] : part[1]], col0 + part[0]
-            m0, m1 = col0 // PACK, (col0 + piece.shape[2]) // PACK
+        def round_loadings(copy, a, b, col0, planes=ALL_PLANES, cols=None):
+            piece, (t0, t1) = l_raw[a, b, col0], planes
+            first, last = cols or (0, piece.shape[2])
+            m0, m1 = (col0 + first) // PACK, (col0 + last) // PACK
             copy(
                 l_rounded[a, b][:].rearrange("p (t m i) -> p m i t", t=PACK, i=PACK)[:, m0:m1, :, t0:t1],
-                piece.rearrange("p i (m t) -> p m i t", t=PACK)[:, :, :, t0:t1],
+                piece[:, :, first:last].rearrange("p i (m t) -> p m i t", t=PACK)[:, :, :, t0:t1],
             )
 
         def quantise_loadings(a, b, planes):
@@ -139,7 +134,7 @@ def tile_list_scenario_profit_store_kernel(
                         out=r_sums[b, c, t],
                         lhsT=l_codes[a, b][:, P * t : P * (t + 1)].bitcast(FP8X4),
                         lhsT_scale=l_scales[a, b][:, P * t : P * (t + 1)],
-                        rhs=v_codes[a, c].bitcast(FP8X4),
+                        rhs=v_words[a][:, CHUNK * c : CHUNK * (c + 1)].bitcast(FP8X4),
                         rhs_scale=v_scales[4 * a : P, CHUNK * c : CHUNK * (c + 1)],
                         start=(a == 0),
                         stop=(a == 1),
@@ -210,19 +205,18 @@ def tile_list_scenario_profit_store_kernel(
                             stop=(b == 1 and j0 == P),
                         )
 
+        def scatter(n, j0, y):
+            j1 = j0 + y.shape[1]
+            entries = scatter_list[:, j0 // GROUP : j1 // GROUP]
+            nc.vector.tensor_tensor(windows[n][:].indirect(entries), y, wgo_sb[:, j0:j1], ALU.mult)
+
         def place_results(tiles, c, over=None):
             y_sums = y_place[tiles, c]
-            width, j0 = y_sums.shape[1] // len(tiles), CHUNK * c
+            width = y_sums.shape[1] // len(tiles)
             y_sb = sb([P, y_sums.shape[1]], F32, "y_sb%d%d" % (tiles[0], c), over)
             nc.scalar.copy(y_sb[:], y_sums)
-            entries = scatter_list[:, j0 // GROUP : (j0 + width) // GROUP]
             for place, n in enumerate(tiles):
-                nc.vector.tensor_tensor(
-                    windows[n][:].indirect(entries),
-                    y_sb[:, width * place : width * (place + 1)],
-                    wgo_sb[:, j0 : j0 + width],
-                    ALU.mult,
-                )
+                scatter(n, CHUNK * c, y_sb[:, width * place : width * (place + 1)])
 
         def store(n):
             queue = nc.scalar if n % 2 else nc.sync
@@ -232,14 +226,12 @@ def tile_list_scenario_profit_store_kernel(
         late_scales = [sb([P, 2 * CHUNK], U8, "late_scales%d" % b) for b in range(2)]
         for b in range(2):
             for c in range(2):
-                h_scales[b, c] = sb([P, CHUNK], U8, "h_scales%d%d" % (b, c))[:]
-                h_scales[b, c + 2] = late_scales[b][:, CHUNK * c : CHUNK * (c + 1)]
-                h_codes[b, c + 2] = late_codes[b][:, CHUNK * c : CHUNK * (c + 1)]
-        for b in range(2):
-            for c in range(2):
                 h_codes[b, c] = sb([P, CHUNK], U32, "h_codes%d%d" % (b, c))[:]
+                h_scales[b, c] = sb([P, CHUNK], U8, "h_scales%d%d" % (b, c))[:]
+                h_codes[b, c + 2] = late_codes[b][:, CHUNK * c : CHUNK * (c + 1)]
+                h_scales[b, c + 2] = late_scales[b][:, CHUNK * c : CHUNK * (c + 1)]
 
-        gather(v_pass0[:], tab_w[0][:].bitcast(U32), 0, S)
+        gather_words(0, 0, S)
         last_window = sb([P, T2], F32, "window3", over="tab_w0")
         nc.gpsimd.memset(last_window[:], 0.0)
         round_loadings(on_scalar, 0, 0, 0)
@@ -250,9 +242,9 @@ def tile_list_scenario_profit_store_kernel(
         round_loadings(on_scalar, 1, 0, 0, HIGH_PLANES, (0, HALF_COLS))
         round_loadings(on_vector, 1, 0, 0, HIGH_PLANES, (HALF_COLS, PASS))
         quantise_loadings(1, 0, LOW_PLANES)
-        gather_second_pass(0)
+        gather_words(1, 0, CHUNK)
         quantise_loadings(1, 0, HIGH_PLANES)
-        gather(v_pass1[:, CHUNK:], tab_w[1][:].bitcast(U32), CHUNK, S)
+        gather_words(1, CHUNK, S)
         log_returns(0, 0, (0, 1, 2, 3))
         round_loadings(on_scalar, 0, 1, 0)
         exponentials(0, 0)
@@ -285,18 +277,27 @@ def tile_list_scenario_profit_store_kernel(
             interleave(on_vector, 1, 0, j0, j0 + P)
         for j0 in (0, P):
             quantise_profit(1, 0, j0, j0 + P)
-        interleave(on_vector, 0, 1, over="h_rounded10_0")
-        quantise_profit(0, 1)
-        windows.extend([sb([P, T2], F32, "window2", over="h_rounded10_0"), last_window])
+        for j0 in (0, P):
+            interleave(on_vector, 0, 1, j0, j0 + P, over="h_rounded10_%d" % j0)
+        for j0 in (0, P):
+            quantise_profit(0, 1, j0, j0 + P)
+        windows.extend([sb([P, T2], F32, "window2", over="h_rounded10_%d" % P), last_window])
         nc.gpsimd.memset(windows[2][:], 0.0)
         log_returns(1, 1, (4, 5), order=(2, 0, 3, 1))
         exponentials(1, 1, over="growth00_0")
-        portfolios((0,), 0, 0)
+        first_sums = sb([P, CHUNK], F32, "first_sums")
+        first_places = ((0, banks[0][:, :P]), (P, banks[1][:, :P]))
+        for j0, place in first_places:
+            for b in range(2):
+                codes, scales = h_codes[b, 0][:, j0 : j0 + P], h_scales[b, 0][:, j0 : j0 + P]
+                second_product(place, 0, b, codes, scales, start=(b == 0), stop=(b == 1))
         portfolios((1,), 0, 6)
         portfolios((2, 3), 0, 4)
         log_returns(1, 2, (2, 3))
         profit_on_scalar(1, 1)
-        place_results((0,), 0)
+        for j0, place in first_places:
+            nc.scalar.copy(first_sums[:, j0 : j0 + P], place)
+        scatter(0, 0, first_sums[:])
         place_results((1,), 0)
 
         exponentials(0, 2, HIGH_PLANES, over="h_codes00")

from contextlib import ExitStack

import concourse.mybir as mybir

K, T, H, N, S, T2 = 1024, 2048, 1024, 512, 1024, 2048
FLOPS = 2 * K * H * S + 2 * H * N * S

F32 = mybir.dt.float32
BF16 = mybir.dt.bfloat16
I32 = mybir.dt.int32
U32 = mybir.dt.uint32
U16 = mybir.dt.uint16
U8 = mybir.dt.uint8
FP8X4 = mybir.dt.float8_e4m3fn_x4
FP4X4 = mybir.dt.float4_e2m1fn_x4
ALU = mybir.AluOpType
ACT = mybir.ActivationFunctionType

P = 128
PACK = 4
PASS = P * PACK
BANK = 512
GROUP = 16
CHUNK = 256
LINE = 4
HALF_COLS, LAST_COLS = PASS // 2, PASS - P
ALL_PLANES, LOW_PLANES, HIGH_PLANES = (0, 4), (0, 2), (2, 4)


def tile_list_scenario_profit_store_kernel(
    tc, tab_words, tab_scales, offs, load, drift, price, w4_words, w4_scales, wgo, offs2, out
):
    nc = tc.nc
    on_scalar, on_vector = nc.scalar.copy, nc.vector.tensor_copy
    with ExitStack() as ctx:
        keep = ctx.enter_context(tc.tile_pool(name="keep", bufs=1))
        psum = ctx.enter_context(tc.psum_pool(name="psum", bufs=1))

        def sb(shape, dtype, name, over=None):
            return keep.tile(shape, dtype, name=name, tag=over or name, align_bytes=64)

        gather_list = sb([P, S // GROUP], U16, "gather_list")
        scatter_list = sb([P, S // GROUP], U16, "scatter_list")
        tab_w = [sb([P, T], I32, "tab_w%d" % a) for a in range(2)]
        tab_s = sb([P, T], U8, "tab_s")
        v_words = [sb([P, S], U32, "v_words%d" % a) for a in range(2)]
        v_scales = sb([P, S], U8, "v_scales")
        l_rounded = {ab: sb([P, PACK * PASS], BF16, "l_rounded%d%d" % ab) for ab in ((0, 0), (0, 1), (1, 0))}
        l_codes = {ab: sb([P, PASS], U32, "l_codes%d%d" % ab) for ab in ((0, 1), (1, 0), (1, 1))}
        l_scales = {(a, b): sb([P, PASS], U8, "l_scales%d%d" % (a, b)) for a in range(2) for b in range(2)}
        drift_sb = sb([P, 2, PACK], F32, "drift_sb")
        price_sb = sb([P, 2, PACK], F32, "price_sb")
        minus_price = sb([P, 2, PACK], F32, "minus_price")
        w4_w = sb([P, 2, 2 * N], U8, "w4_w")
        w4_s = sb([P, 2, N], U8, "w4_s")
        wgo_sb = sb([P, S], F32, "wgo_sb")
        windows = [sb([P, T2], F32, "window%d" % n) for n in range(2)]
        banks = [psum.tile([P, BANK], F32, name="bank%d" % i) for i in range(8)]
        l_raw, r_sums, growth, h_planes, h_rounded, h_codes, h_scales, y_place = ({} for i in range(8))

        nc.vector.memset(tab_s[:].bitcast(I32), 0)
        nc.vector.memset(w4_s[:].rearrange("p b n -> p (b n)").bitcast(I32), 0)
        for window in windows:
            nc.vector.memset(window[:], 0.0)

        def load_table(a):
            nc.sync.dma_start(tab_w[a][:], tab_words[a].rearrange("p t i -> p (t i)").bitcast(I32))

        def load_table_scales(rows):
            for r in rows:
                for a in range(2):
                    nc.sync.dma_start(
                        tab_s[4 * a + r : P : 32, :].bitcast(I32), tab_scales[a, r : 16 : 4, :].bitcast(I32)
                    )

        def load_loadings(a, b, col0, col1):
            l_raw[a, b, col0] = sb([P, PACK, col1 - col0], F32, "l_raw%d%d_%d" % (a, b, col0))
            rows = load[PASS * a : PASS * (a + 1), PASS * b + col0 : PASS * b + col1]
            nc.sync.dma_start(l_raw[a, b, col0][:], rows.rearrange("(p i) c -> p i c", i=PACK))

        load_table(0)
        nc.sync.dma_start(gather_list[:], offs)
        load_table_scales((0, 1))
        load_loadings(0, 0, 0, PASS)
        load_table_scales((2, 3))
        load_loadings(1, 0, 0, PASS)
        load_table(1)
        load_loadings(0, 1, 0, HALF_COLS)
        nc.sync.dma_start(drift_sb[:], drift.rearrange("(b p t) -> p b t", b=2, t=PACK))
        load_loadings(0, 1, HALF_COLS, PASS)
        nc.sync.dma_start(price_sb[:], price.rearrange("(b p t) -> p b t", b=2, t=PACK))
        load_loadings(1, 1, 0, HALF_COLS)
        load_loadings(1, 1, HALF_COLS, LAST_COLS)
        load_loadings(1, 1, LAST_COLS, PASS)
        nc.sync.dma_start(wgo_sb[:], wgo)
        nc.sync.dma_start(scatter_list[:], offs2)
        nc.sync.dma_start(w4_w[:].bitcast(I32), w4_words.rearrange("b p c -> p b c").bitcast(I32))
        for r in range(4):
            nc.sync.dma_start(
                w4_s[r:P:32, :, :].bitcast(I32),
                w4_scales[:, r:16:4, :].rearrange("b q n -> q b n").bitcast(I32),
            )

        def gather(dst, window, j0, j1):
            nc.vector.tensor_copy(dst, window.indirect(gather_list[:, j0 // GROUP : j1 // GROUP]))

        def gather_words(a, j0, j1):
            gather(v_words[a][:, j0:j1], tab_w[a][:].bitcast(U32), j0, j1)

        def round_loadings(copy, a, b, col0, planes=ALL_PLANES, cols=None):
            piece, (t0, t1) = l_raw[a, b, col0], planes
            first, last = cols or (0, piece.shape[2])
            m0, m1 = (col0 + first) // PACK, (col0 + last) // PACK
            copy(
                l_rounded[a, b][:].rearrange("p (t m i) -> p m i t", t=PACK, i=PACK)[:, m0:m1, :, t0:t1],
                piece[:, :, first:last].rearrange("p i (m t) -> p m i t", t=PACK)[:, :, :, t0:t1],
            )

        def quantise_loadings(a, b, planes):
            t0, t1 = planes
            nc.vector.quantize_mx(
                out=l_codes[a, b][:, P * t0 : P * t1].bitcast(FP8X4),
                scales=l_scales[a, b][:, P * t0 : P * t1],
                in_=l_rounded[a, b][:, PASS * t0 : PASS * t1],
            )

        def log_returns(b, c, used, order=(0, 1, 2, 3)):
            share = PACK // len(used)
            for k, t in enumerate(order):
                place = CHUNK * (k % share)
                r_sums[b, c, t] = banks[used[k // share]][:, place : place + CHUNK]
                for a in range(2):
                    nc.tensor.matmul_mx(
                        out=r_sums[b, c, t],
                        lhsT=l_codes[a, b][:, P * t : P * (t + 1)].bitcast(FP8X4),
                        lhsT_scale=l_scales[a, b][:, P * t : P * (t + 1)],
                        rhs=v_words[a][:, CHUNK * c : CHUNK * (c + 1)].bitcast(FP8X4),
                        rhs_scale=v_scales[4 * a : P, CHUNK * c : CHUNK * (c + 1)],
                        start=(a == 0),
                        stop=(a == 1),
                    )

        def exponentials(b, c, planes=ALL_PLANES, over=None):
            t0, t1 = planes
            dst = sb([P, t1 - t0, CHUNK], F32, "growth%d%d_%d" % (b, c, t0), over)
            for t in range(t0, t1):
                growth[b, c, t] = dst[:, t - t0, :]
                nc.scalar.activation(growth[b, c, t], r_sums[b, c, t], ACT.Exp, bias=drift_sb[:, b, t : t + 1])

        def profit_on_scalar(b, c, over=None):
            h_planes[b, c] = sb([P, PACK, CHUNK], BF16, "h_planes%d%d" % (b, c), over)
            for t in range(PACK):
                nc.scalar.activation(
                    h_planes[b, c][:, t, :],
                    growth[b, c, t],
                    ACT.Identity,
                    bias=minus_price[:, b, t : t + 1],
                    scale=price_sb[:, b, t : t + 1],
                )

        def profit_on_vector(b, c, dst):
            h_planes[b, c] = dst
            for t in range(PACK):
                nc.vector.tensor_scalar(
                    dst[:, t, :], growth[b, c, t], -1.0, price_sb[:, b, t : t + 1], ALU.add, ALU.mult
                )

        def interleave(copy, b, c, j0=0, j1=CHUNK, over=None):
            h_rounded[b, c, j0] = sb([P, (j1 - j0) * PACK], BF16, "h_rounded%d%d_%d" % (b, c, j0), over)[:]
            copy(
                h_rounded[b, c, j0].rearrange("p (g e t) -> p g t e", e=LINE, t=PACK),
                h_planes[b, c][:, :, j0:j1].rearrange("p t (g e) -> p g t e", e=LINE),
            )

        def quantise_profit(b, c, j0=0, j1=CHUNK):
            nc.vector.quantize_mx(
                out=h_codes[b, c][:, j0:j1].bitcast(FP8X4),
                scales=h_scales[b, c][:, j0:j1],
                in_=h_rounded[b, c, j0],
            )

        def second_product(dst, n, b, codes, scales, start, stop):
            nc.tensor.matmul_mx(
                out=dst,
                lhsT=w4_w[:, b, 2 * P * n : 2 * P * (n + 1)].bitcast(FP4X4),
                lhsT_scale=w4_s[:, b, P * n : P * (n + 1)],
                rhs=codes.bitcast(FP8X4),
                rhs_scale=scales,
                start=start,
                stop=stop,
            )

        def portfolios(tiles, c, bank):
            y_place[tiles, c] = banks[bank][:, : CHUNK * len(tiles)]
            for place, n in enumerate(tiles):
                for b in range(2):
                    for j0 in (0, P):
                        second_product(
                            banks[bank][:, CHUNK * place + j0 : CHUNK * place + j0 + P],
                            n,
                            b,
                            h_codes[b, c][:, j0 : j0 + P],
                            h_scales[b, c][:, j0 : j0 + P],
                            start=(b == 0 and j0 == 0),
                            stop=(b == 1 and j0 == P),
                        )

        def scatter(n, j0, y):
            j1 = j0 + y.shape[1]
            entries = scatter_list[:, j0 // GROUP : j1 // GROUP]
            nc.vector.tensor_tensor(windows[n][:].indirect(entries), y, wgo_sb[:, j0:j1], ALU.mult)

        def place_results(tiles, c, over=None):
            y_sums = y_place[tiles, c]
            width = y_sums.shape[1] // len(tiles)
            y_sb = sb([P, y_sums.shape[1]], F32, "y_sb%d%d" % (tiles[0], c), over)
            nc.scalar.copy(y_sb[:], y_sums)
            for place, n in enumerate(tiles):
                scatter(n, CHUNK * c, y_sb[:, width * place : width * (place + 1)])

        def store(n):
            queue = nc.scalar if n % 2 else nc.sync
            queue.dma_start(out[P * n : P * (n + 1), :], windows[n][:])

        late_codes = [sb([P, 2 * CHUNK], U32, "late_codes%d" % b) for b in range(2)]
        late_scales = [sb([P, 2 * CHUNK], U8, "late_scales%d" % b) for b in range(2)]
        for b in range(2):
            for c in range(2):
                h_codes[b, c] = sb([P, CHUNK], U32, "h_codes%d%d" % (b, c))[:]
                h_scales[b, c] = sb([P, CHUNK], U8, "h_scales%d%d" % (b, c))[:]
                h_codes[b, c + 2] = late_codes[b][:, CHUNK * c : CHUNK * (c + 1)]
                h_scales[b, c + 2] = late_scales[b][:, CHUNK * c : CHUNK * (c + 1)]

        gather_words(0, 0, S)
        last_window = sb([P, T2], F32, "window3", over="tab_w0")
        nc.gpsimd.memset(last_window[:], 0.0)
        round_loadings(on_scalar, 0, 0, 0)
        gather(v_scales[:], tab_s[:], 0, S)
        l_codes[0, 0] = sb([P, PASS], U32, "l_codes00", over="tab_s")
        quantise_loadings(0, 0, ALL_PLANES)
        round_loadings(on_scalar, 1, 0, 0, LOW_PLANES)
        round_loadings(on_scalar, 1, 0, 0, HIGH_PLANES, (0, HALF_COLS))
        round_loadings(on_vector, 1, 0, 0, HIGH_PLANES, (HALF_COLS, PASS))
        quantise_loadings(1, 0, LOW_PLANES)
        gather_words(1, 0, CHUNK)
        quantise_loadings(1, 0, HIGH_PLANES)
        gather_words(1, CHUNK, S)
        log_returns(0, 0, (0, 1, 2, 3))
        round_loadings(on_scalar, 0, 1, 0)
        exponentials(0, 0)
        nc.scalar.activation(minus_price[:], price_sb[:], ACT.Identity, scale=-1.0)
        log_returns(0, 1, (4, 5))
        exponentials(0, 1)
        profit_on_scalar(0, 1)
        log_returns(0, 2, (6, 7))
        exponentials(0, 2, LOW_PLANES)

        round_loadings(on_vector, 0, 1, HALF_COLS, LOW_PLANES)
        round_loadings(on_vector, 0, 1, HALF_COLS, HIGH_PLANES)
        quantise_loadings(0, 1, LOW_PLANES)
        quantise_loadings(0, 1, HIGH_PLANES)
        l_rounded[1, 1] = sb([P, PACK * PASS], BF16, "l_rounded11", over="l_raw01_%d" % HALF_COLS)
        round_loadings(on_vector, 1, 1, 0)
        round_loadings(on_vector, 1, 1, HALF_COLS)
        round_loadings(on_vector, 1, 1, LAST_COLS, LOW_PLANES)
        round_loadings(on_vector, 1, 1, LAST_COLS, HIGH_PLANES)
        for planes in ((0, 1), (1, 2), HIGH_PLANES):
            quantise_loadings(1, 1, planes)

        profit_on_vector(0, 0, l_rounded[1, 1][:, : 2 * PASS].rearrange("p (t j) -> p t j", t=PACK))
        interleave(on_vector, 0, 0)
        log_returns(1, 0, (0, 1, 2, 3))
        exponentials(1, 0)
        profit_on_vector(1, 0, sb([P, PACK, CHUNK], BF16, "h_planes10"))
        quantise_profit(0, 0)
        for j0 in (0, P):
            interleave(on_vector, 1, 0, j0, j0 + P)
        for j0 in (0, P):
            quantise_profit(1, 0, j0, j0 + P)
        for j0 in (0, P):
            interleave(on_vector, 0, 1, j0, j0 + P, over="h_rounded10_%d" % j0)
        for j0 in (0, P):
            quantise_profit(0, 1, j0, j0 + P)
        windows.extend([sb([P, T2], F32, "window2", over="h_rounded10_%d" % P), last_window])
        nc.gpsimd.memset(windows[2][:], 0.0)
        log_returns(1, 1, (4, 5), order=(2, 0, 3, 1))
        exponentials(1, 1, over="growth00_0")
        first_sums = sb([P, CHUNK], F32, "first_sums")
        first_places = ((0, banks[0][:, :P]), (P, banks[1][:, :P]))
        for j0, place in first_places:
            for b in range(2):
                codes, scales = h_codes[b, 0][:, j0 : j0 + P], h_scales[b, 0][:, j0 : j0 + P]
                second_product(place, 0, b, codes, scales, start=(b == 0), stop=(b == 1))
        portfolios((1,), 0, 6)
        portfolios((2, 3), 0, 4)
        log_returns(1, 2, (2, 3))
        profit_on_scalar(1, 1)
        for j0, place in first_places:
            nc.scalar.copy(first_sums[:, j0 : j0 + P], place)
        scatter(0, 0, first_sums[:])
        place_results((1,), 0)

        exponentials(0, 2, HIGH_PLANES, over="h_codes00")
        log_returns(0, 3, (7, 6))
        interleave(on_scalar, 1, 1, over="h_codes10")
        quantise_profit(1, 1)
        portfolios((0, 1), 1, 5)
        portfolios((2, 3), 1, 1)
        place_results((2, 3), 0, over="h_planes11")

        profit_on_scalar(0, 2, over="h_scales10")
        interleave(on_scalar, 0, 2)
        quantise_profit(0, 2)
        exponentials(1, 2, over="h_scales00")
        log_returns(1, 3, (2, 3))
        place_results((0, 1), 1, over="h_scales10")
        profit_on_scalar(1, 2)
        interleave(on_scalar, 1, 2)
        quantise_profit(1, 2)
        portfolios((0, 1), 2, 0)
        portfolios((2,), 2, 4)
        place_results((2, 3), 1, over="h_planes12")

        exponentials(0, 3, over="h_codes00")
        profit_on_scalar(0, 3)
        interleave(on_scalar, 0, 3)
        quantise_profit(0, 3)
        exponentials(1, 3, LOW_PLANES, over="h_scales00")
        place_results((0, 1), 2, over="h_planes03")
        exponentials(1, 3, HIGH_PLANES)
        profit_on_scalar(1, 3)
        interleave(on_scalar, 1, 3)
        quantise_profit(1, 3)
        portfolios((0,), 3, 5)
        portfolios((1, 2), 3, 1)

        place_results((2,), 2, over="h_planes13")
        place_results((0,), 3)
        store(0)
        place_results((1, 2), 3)
        store(1)
        store(2)
        for b in range(2):
            second_product(banks[1][:], 3, b, late_codes[b][:], late_scales[b][:], start=(b == 0), stop=(b == 1))
        y_place[(3,), 2] = banks[1][:]
        place_results((3,), 2)
        store(3)
